import numpy as np
import ml_dtypes


def mxq(x, axis, fmt="e4m3"):
    dtype, down = {"e4m3": (ml_dtypes.float8_e4m3fn, 7), "e5m2": (ml_dtypes.float8_e5m2, 14)}[fmt]
    v = np.moveaxis(np.asarray(x, np.float32).astype(ml_dtypes.bfloat16).astype(np.float64), axis, -1)
    blocks = v.reshape(v.shape[:-1] + (-1, 32))
    amax = np.abs(blocks).max(-1, keepdims=True)
    byte = np.maximum(np.where(amax > 0, np.frexp(amax)[1] - 1 + 127, 0) - down, 1)
    scale = np.exp2(byte - 127.0)
    codes = (blocks / scale).astype(np.float32).astype(dtype).astype(np.float64)
    return np.moveaxis((codes * scale).reshape(v.shape), -1, axis)


WIDE = False


def mx_kscale(k):
    if not WIDE:
        return np.ones(k)
    levels = np.array([10, -10, 5, -5, 0])
    if k % 512:
        return np.exp2(np.random.permutation(np.resize(levels, k // 32))).repeat(32)
    a = np.empty((k // 512, 16))
    for p in range(k // 512):
        a[p, :8] = np.random.permutation(np.resize(levels, 8))
        for g in range(8):
            far = levels[np.abs(levels - a[p, g]) >= 10]
            a[p, g + 8] = far[np.random.randint(len(far))]
    return np.exp2(a.ravel()).repeat(32)


def f64(x):
    return np.asarray(x).astype(np.float64)


def striped(idx):
    return np.tile(idx.reshape(-1, 16).T, (8, 1)).astype(np.uint16)


def unstriped(offs):
    return offs[:16].T.reshape(-1).astype(np.int64)


E2M1 = np.array([0.0, 0.5, 1.0, 1.5, 2.0, 3.0, 4.0, 6.0, -0.0, -0.5, -1.0, -1.5, -2.0, -3.0, -4.0, -6.0])


def pack_weight(w, fmt):
    k, n = w.shape
    w = f64(np.asarray(w, np.float32).astype(ml_dtypes.bfloat16)).reshape(k // 32, 32, n)
    amax = np.abs(w).max(1)
    if fmt == "e4m3":
        byte = np.frexp(amax)[1] - 1 + 127 - 7
    else:
        mant, ex = np.frexp(amax / 6.0)
        byte = np.where(mant > 0.5, ex, ex - 1) + 127
    byte = np.clip(np.where(amax > 0, byte, 1), 1, 254)
    scaled = (w * np.exp2(127.0 - byte)[:, None, :]).reshape(k, n).astype(np.float32)
    by_word = np.ascontiguousarray(scaled.reshape(k // 512, 128, 4, n).transpose(0, 1, 3, 2))
    if fmt == "e4m3":
        words = by_word.astype(ml_dtypes.float8_e4m3fn).view(np.uint8)
    else:
        c = by_word.astype(ml_dtypes.float4_e2m1fn).view(np.uint8) & 0xF
        words = (c[..., 0::2] | (c[..., 1::2] << 4)).reshape(k // 512, 128, 2 * n)
    return np.ascontiguousarray(words), np.ascontiguousarray(byte.astype(np.uint8).reshape(k // 512, 16, n))


def unpack_weight(words, scales, fmt):
    g, _, n = scales.shape
    words = np.ascontiguousarray(words).reshape(g, 128, n, -1)
    if fmt == "e4m3":
        vals = words.view(ml_dtypes.float8_e4m3fn).astype(np.float64)
    else:
        nib = np.empty((g, 128, n, 4), np.uint8)
        nib[..., 0::2] = words & 0xF
        nib[..., 1::2] = words >> 4
        vals = E2M1[nib]
    vals = vals * np.repeat(np.exp2(scales.astype(np.float64) - 127.0), 8, axis=1)[..., None]
    return vals.transpose(0, 1, 3, 2).reshape(g * 512, n)


def silu(v):
    return v / (1.0 + np.exp(-np.maximum(v, -700.0)))


K, T, E, C, H, N = 1536, 768, 8, 128, 512, 128
TOP = 4
PAD = 64


def by_expert(wq, xq):
    return np.concatenate([wq[e].T @ xq[:, e * C:(e + 1) * C] for e in range(E)], axis=1)


def setup_inputs():
    n = np.random.standard_normal
    s = mx_kscale(K)[:, None]
    u = mx_kscale(H)
    slot_token = np.empty(E * C, np.int64); pos = np.tile(E * C + np.arange(T) % PAD, (TOP, 1)); taken = np.zeros(T, np.int64)
    liked = np.random.randn(T)
    for e in np.random.permutation(E):
        free = np.flatnonzero(taken < TOP); pick = np.random.permutation(free[np.argsort(-(liked[free] + np.random.gumbel(size=free.size)))[:C]]); slot_token[e * C:(e + 1) * C] = pick
        pos[taken[pick], pick] = e * C + np.arange(C); taken[pick] += 1
    g = np.random.uniform(0.2, 0.8, (TOP, T))
    x = pack_weight(n((K, T)) * s, "e4m3")
    return {
        "x_words": x[0],
        "x_scales": x[1],
        "w1": (n((E, K, H)) / np.sqrt(K) / s[None] * u[None, None, :]).astype(np.float32),
        "w2": (n((E, H, N)) / np.sqrt(H) / u[None, :, None]).astype(np.float32),
        "gate": np.stack([np.tile(r, (N, 1)) for r in g]).astype(np.float32),
        "offs": striped(slot_token),
        "pos1": striped(pos[0]),
        "pos2": striped(pos[1]),
        "pos3": striped(pos[2]),
        "pos4": striped(pos[3]),
    }


def reference(x_words, x_scales, w1, w2, gate, offs, pos1, pos2, pos3, pos4):
    idx = unstriped(offs)
    xq = unpack_weight(x_words, x_scales, "e4m3")[:, idx]
    h = silu(by_expert(mxq(f64(w1), 1, "e4m3"), xq))
    y = by_expert(mxq(f64(w2), 1, "e4m3"), mxq(h, 0, "e4m3"))
    y = np.concatenate([y, np.zeros((N, PAD))], axis=1)
    return sum(f64(gate[r]) * y[:, unstriped(p)] for r, p in enumerate((pos1, pos2, pos3, pos4)))

@@ -1,0 +1,182 @@
+from contextlib import ExitStack
+
+import concourse.mybir as mybir
+
+K, T, E, C, H, N = 1536, 768, 8, 128, 512, 128
+TOP = 4
+PAD = 64
+SLOTS = E * C
+FLOPS = 2 * SLOTS * (K * H + H * N)
+
+F32 = mybir.dt.float32
+BF16 = mybir.dt.bfloat16
+I32 = mybir.dt.int32
+U32 = mybir.dt.uint32
+U16 = mybir.dt.uint16
+U8 = mybir.dt.uint8
+FP8X4 = mybir.dt.float8_e4m3fn_x4
+MULT = mybir.AluOpType.mult
+ADD = mybir.AluOpType.add
+SILU = mybir.ActivationFunctionType.Silu
+
+P = 128
+PACK = 4
+PASSES = K // (P * PACK)
+LIST_ROWS = 16
+GATHER = 256
+STREAM_BUFS = 12
+VECTOR_M = 60
+EARLY_W2 = ((0, 1),)
+LATE_W2 = ((2, 3), (4, 5), (6,), (7,))
+TOKEN_CUTS = (0, 512, 640, 768)
+TAIL = [(w[0], int(w[1]), int(w[2])) for w in "g00 g01 g02 a01 g03 a02 g10 a03 g20 g11 g21 g12 a11 g22 a21 g13 a12 g23 a22 a13 a23".split()]
+
+
+def tile_moe_ecr_mlp_silu_kernel(
+    tc, x_words, x_scales, w1, w2, gate, offs, pos1, pos2, pos3, pos4, out
+):
+    nc = tc.nc
+    with ExitStack() as ctx:
+        lists = ctx.enter_context(tc.tile_pool(name="lists", bufs=1))
+        keep = ctx.enter_context(tc.tile_pool(name="keep", bufs=1))
+        stream = ctx.enter_context(tc.tile_pool(name="stream", bufs=STREAM_BUFS))
+        rounded = ctx.enter_context(tc.tile_pool(name="rounded", bufs=4))
+        coded = ctx.enter_context(tc.tile_pool(name="coded", bufs=6))
+        psum_a = ctx.enter_context(tc.psum_pool(name="psum_a", bufs=3))
+        psum_y = ctx.enter_context(tc.psum_pool(name="psum_y", bufs=4))
+
+        token_scales = keep.tile([P, T], U8, name="token_scales", align_bytes=64)
+        nc.vector.memset(token_scales[:].bitcast(I32), 0)
+        for quad in range(4):
+            nc.scalar.dma_start(
+                out=token_scales[32 * quad : 32 * quad + 4 * PASSES, :].bitcast(I32),
+                in_=x_scales[:, 4 * quad : 4 * quad + 4, :].bitcast(I32),
+            )
+
+        token_words = keep.tile([P, PASSES, T], I32, name="token_words", align_bytes=64)
+        nc.sync.dma_start(out=token_words[:], in_=x_words.rearrange("o p t r -> p o (t r)").bitcast(I32))
+        slot_list = lists.tile([P, SLOTS // LIST_ROWS], U16, name="slot_list")
+        nc.sync.dma_start(slot_list[:], offs)
+
+        y = keep.tile([P, SLOTS + PAD], F32, name="y", align_bytes=64)
+        nc.vector.memset(y[:, SLOTS:], 0.0)
+
+        slot_words, slot_scales, h_codes, h_scales = {}, {}, {}, {}
+
+        def gather_tokens(g):
+            cols = slice(g * GATHER // LIST_ROWS, (g + 1) * GATHER // LIST_ROWS)
+            words = keep.tile([P, PASSES, GATHER], U32, name="slot_words%d" % g, align_bytes=64)
+            scales = keep.tile([P, GATHER], U8, name="slot_scales%d" % g, align_bytes=64)
+            for o in range(PASSES):
+                nc.vector.tensor_copy(words[:, o, :], token_words[:, o, :].bitcast(U32).indirect(slot_list[:, cols]))
+            nc.vector.tensor_copy(scales[:], token_scales[:].indirect(slot_list[:, cols]))
+            slot_words[g], slot_scales[g] = words, scales
+
+        def first_layer(e):
+            g, first = divmod(e * C, GATHER)
+            slots = slice(first, first + C)
+            acc = psum_a.tile([P, PACK, C], F32, name="acc")
+            for o in range(PASSES):
+                raw = stream.tile([P, PACK, H], F32, name="raw", tag="stream")
+                nc.sync.dma_start(
+                    out=raw[:], in_=w1[e, o * P * PACK : (o + 1) * P * PACK, :].rearrange("(p j) c -> p j c", j=PACK)
+                )
+                w_bf = rounded.tile([P, H * PACK], BF16, name="w1_bf", align_bytes=64)
+                dst = w_bf[:].rearrange("p (t m j) -> p m j t", t=PACK, j=PACK)
+                src = raw[:].rearrange("p j (m t) -> p m j t", t=PACK)
+                nc.vector.tensor_copy(out=dst[:, :VECTOR_M], in_=src[:, :VECTOR_M])
+                nc.scalar.copy(out=dst[:, VECTOR_M:], in_=src[:, VECTOR_M:])
+                codes = coded.tile([P, H], U32, name="w1_codes", align_bytes=64)
+                scales = coded.tile([P, H], U8, name="w1_scales", align_bytes=64)
+                nc.vector.quantize_mx(out=codes[:].bitcast(FP8X4), scales=scales[:], in_=w_bf[:])
+                for t in range(PACK):
+                    cols = slice(t * P, (t + 1) * P)
+                    nc.tensor.matmul_mx(
+                        out=acc[:, t, :],
+                        lhsT=codes[:, cols].bitcast(FP8X4),
+                        lhsT_scale=scales[:, cols],
+                        rhs=slot_words[g][:, o, slots].bitcast(FP8X4),
+                        rhs_scale=slot_scales[g][4 * o :, slots],
+                        start=(o == 0 and t == 0),
+                        stop=(o == PASSES - 1 and t == PACK - 1),
+                    )
+            h_bf = rounded.tile([P, C, PACK], BF16, name="h_bf", align_bytes=64)
+            nc.scalar.activation(out=h_bf[:], in_=acc[:].rearrange("p t s -> p s t"), func=SILU)
+            h_codes[e] = keep.tile([P, C], U32, name="h_codes%d" % e, align_bytes=64)
+            h_scales[e] = keep.tile([P, C], U8, name="h_scales%d" % e, align_bytes=64)
+            nc.vector.quantize_mx(
+                out=h_codes[e][:].bitcast(FP8X4), scales=h_scales[e][:], in_=h_bf[:].rearrange("p s t -> p (s t)")
+            )
+
+        def load_w2(experts):
+            raw = stream.tile([P, len(experts), PACK * N], F32, name="raw2", tag="stream")
+            nc.sync.dma_start(
+                out=raw[:], in_=w2[experts[0] : experts[-1] + 1].rearrange("e (p j) n -> p e (j n)", j=PACK)
+            )
+            return raw
+
+        def second_layer(experts, raw, copy):
+            for i, e in enumerate(experts):
+                w_bf = rounded.tile([P, N * PACK], BF16, name="w2_bf", align_bytes=64)
+                copy(
+                    out=w_bf[:].rearrange("p (c i j) -> p c j i", i=4, j=PACK),
+                    in_=raw[:, i, :].rearrange("p (j c i) -> p c j i", i=4, j=PACK),
+                )
+                codes = coded.tile([P, N], U32, name="w2_codes", align_bytes=64)
+                scales = coded.tile([P, N], U8, name="w2_scales", align_bytes=64)
+                nc.vector.quantize_mx(out=codes[:].bitcast(FP8X4), scales=scales[:], in_=w_bf[:])
+                acc = psum_y.tile([P, C], F32, name="acc_y")
+                nc.tensor.matmul_mx(
+                    out=acc[:],
+                    lhsT=codes[:].bitcast(FP8X4),
+                    lhsT_scale=scales[:],
+                    rhs=h_codes[e][:].bitcast(FP8X4),
+                    rhs_scale=h_scales[e][:],
+                    start=True,
+                    stop=True,
+                )
+                nc.scalar.copy(out=y[:, e * C : (e + 1) * C], in_=acc[:])
+
+        back_lists = []
+        for e in range(E):
+            if (e * C) % GATHER == 0:
+                gather_tokens(e * C // GATHER)
+            first_layer(e)
+            for experts in EARLY_W2:
+                if experts[-1] == e:
+                    second_layer(experts, load_w2(experts), nc.scalar.copy)
+            if e == 2:
+                for r, pos in enumerate((pos1, pos2, pos3, pos4)):
+                    back = lists.tile([P, T // LIST_ROWS], U16, name="back%d" % r)
+                    nc.sync.dma_start(back[:], pos)
+                    back_lists.append(back)
+        for n, experts in enumerate(LATE_W2):
+            second_layer(experts, load_w2(experts), nc.scalar.copy if n == 0 else nc.vector.tensor_copy)
+
+        gates = []
+        for r in range(TOP):
+            g_tile = stream.tile([P, T], F32, name="gate", tag="stream")
+            nc.sync.dma_start(out=g_tile[:], in_=gate[r])
+            gates.append(g_tile)
+
+        chunks = [(lo, hi) for lo, hi in zip(TOKEN_CUTS[:-1], TOKEN_CUTS[1:])]
+        parts, sums = {}, {}
+
+        def fetch(c, r):
+            lo, hi = chunks[c]
+            part = keep.tile([P, hi - lo], F32, name="part%d_%d" % (c, r))
+            nc.vector.tensor_tensor(
+                part[:], y[:].indirect(back_lists[r][:, lo // LIST_ROWS : hi // LIST_ROWS]), gates[r][:, lo:hi], MULT
+            )
+            parts[c, r] = part
+
+        def add(c, r):
+            lo, hi = chunks[c]
+            total = keep.tile([P, hi - lo], F32, name="sum%d_%d" % (c, r))
+            nc.vector.tensor_tensor(total[:], (parts[c, 0] if r == 1 else sums[c])[:], parts[c, r][:], ADD)
+            sums[c] = total
+            if r == TOP - 1:
+                (nc.sync if c % 2 == 0 else nc.scalar).dma_start(out=out[:, lo:hi], in_=total[:])
+
+        for step, c, r in TAIL:
+            (fetch if step == "g" else add)(c, r)

@@ -26,8 +26,8 @@ LIST_ROWS = 16
 GATHER = 256
 STREAM_BUFS = 12
 VECTOR_M = 60
+LAST_VECTOR_M = 84
 EARLY_W2 = ((0, 1),)
-LATE_W2 = ((2, 3), (4, 5), (6,), (7,))
 TOKEN_CUTS = (0, 512, 640, 768)
 TAIL = [(w[0], int(w[1]), int(w[2])) for w in "g00 g01 g02 a01 g03 a02 g10 a03 g20 g11 g21 g12 a11 g22 a21 g13 a12 g23 a22 a13 a23".split()]
 
@@ -41,7 +41,8 @@ def tile_moe_ecr_mlp_silu_kernel(
         keep = ctx.enter_context(tc.tile_pool(name="keep", bufs=1))
         stream = ctx.enter_context(tc.tile_pool(name="stream", bufs=STREAM_BUFS))
         rounded = ctx.enter_context(tc.tile_pool(name="rounded", bufs=4))
-        coded = ctx.enter_context(tc.tile_pool(name="coded", bufs=6))
+        coded = ctx.enter_context(tc.tile_pool(name="coded", bufs=12))
+        slots_pool = ctx.enter_context(tc.tile_pool(name="slots", bufs=2))
         psum_a = ctx.enter_context(tc.psum_pool(name="psum_a", bufs=3))
         psum_y = ctx.enter_context(tc.psum_pool(name="psum_y", bufs=4))
 
@@ -61,12 +62,12 @@ def tile_moe_ecr_mlp_silu_kernel(
         y = keep.tile([P, SLOTS + PAD], F32, name="y", align_bytes=64)
         nc.vector.memset(y[:, SLOTS:], 0.0)
 
-        slot_words, slot_scales, h_codes, h_scales = {}, {}, {}, {}
+        slot_words, slot_scales, h_codes, h_scales, w1_rounded = {}, {}, {}, {}, {}
 
         def gather_tokens(g):
             cols = slice(g * GATHER // LIST_ROWS, (g + 1) * GATHER // LIST_ROWS)
-            words = keep.tile([P, PASSES, GATHER], U32, name="slot_words%d" % g, align_bytes=64)
-            scales = keep.tile([P, GATHER], U8, name="slot_scales%d" % g, align_bytes=64)
+            words = slots_pool.tile([P, PASSES, GATHER], U32, name="slot_words", align_bytes=64)
+            scales = slots_pool.tile([P, GATHER], U8, name="slot_scales", align_bytes=64)
             for o in range(PASSES):
                 nc.vector.tensor_copy(words[:, o, :], token_words[:, o, :].bitcast(U32).indirect(slot_list[:, cols]))
             nc.vector.tensor_copy(scales[:], token_scales[:].indirect(slot_list[:, cols]))
@@ -82,13 +83,22 @@ def tile_moe_ecr_mlp_silu_kernel(
                     out=raw[:], in_=w1[e, o * P * PACK : (o + 1) * P * PACK, :].rearrange("(p j) c -> p j c", j=PACK)
                 )
                 w_bf = rounded.tile([P, H * PACK], BF16, name="w1_bf", align_bytes=64)
+                w1_rounded[e, o] = w_bf
                 dst = w_bf[:].rearrange("p (t m j) -> p m j t", t=PACK, j=PACK)
                 src = raw[:].rearrange("p j (m t) -> p m j t", t=PACK)
-                nc.vector.tensor_copy(out=dst[:, :VECTOR_M], in_=src[:, :VECTOR_M])
-                nc.scalar.copy(out=dst[:, VECTOR_M:], in_=src[:, VECTOR_M:])
+                last = e == E - 1 and o == PASSES - 1
+                split = LAST_VECTOR_M if last else VECTOR_M
+                nc.vector.tensor_copy(out=dst[:, :split], in_=src[:, :split])
+                nc.scalar.copy(out=dst[:, split:], in_=src[:, split:])
                 codes = coded.tile([P, H], U32, name="w1_codes", align_bytes=64)
                 scales = coded.tile([P, H], U8, name="w1_scales", align_bytes=64)
-                nc.vector.quantize_mx(out=codes[:].bitcast(FP8X4), scales=scales[:], in_=w_bf[:])
+                width = H // 2 if last else H
+                for c0 in range(0, H, width):
+                    nc.vector.quantize_mx(
+                        out=codes[:, c0 : c0 + width].bitcast(FP8X4),
+                        scales=scales[:, c0 : c0 + width],
+                        in_=w_bf[:, c0 * PACK : (c0 + width) * PACK],
+                    )
                 for t in range(PACK):
                     cols = slice(t * P, (t + 1) * P)
                     nc.tensor.matmul_mx(
@@ -108,34 +118,32 @@ def tile_moe_ecr_mlp_silu_kernel(
                 out=h_codes[e][:].bitcast(FP8X4), scales=h_scales[e][:], in_=h_bf[:].rearrange("p s t -> p (s t)")
             )
 
-        def load_w2(experts):
-            raw = stream.tile([P, len(experts), PACK * N], F32, name="raw2", tag="stream")
-            nc.sync.dma_start(
-                out=raw[:], in_=w2[experts[0] : experts[-1] + 1].rearrange("e (p j) n -> p e (j n)", j=PACK)
-            )
-            return raw
-
-        def second_layer(experts, raw, copy):
+        def second_layer(experts, w_bf, copy):
+            count = len(experts)
             for i, e in enumerate(experts):
-                w_bf = rounded.tile([P, N * PACK], BF16, name="w2_bf", align_bytes=64)
+                raw = stream.tile([P, PACK * N], F32, name="raw2", tag="stream")
+                nc.sync.dma_start(out=raw[:], in_=w2[e].rearrange("(p j) n -> p (j n)", j=PACK))
                 copy(
-                    out=w_bf[:].rearrange("p (c i j) -> p c j i", i=4, j=PACK),
-                    in_=raw[:, i, :].rearrange("p (j c i) -> p c j i", i=4, j=PACK),
+                    out=w_bf[:, i * H : (i + 1) * H].rearrange("p (c i j) -> p c j i", i=4, j=PACK),
+                    in_=raw[:].rearrange("p (j c i) -> p c j i", i=4, j=PACK),
                 )
-                codes = coded.tile([P, N], U32, name="w2_codes", align_bytes=64)
-                scales = coded.tile([P, N], U8, name="w2_scales", align_bytes=64)
-                nc.vector.quantize_mx(out=codes[:].bitcast(FP8X4), scales=scales[:], in_=w_bf[:])
-                acc = psum_y.tile([P, C], F32, name="acc_y")
+            codes = coded.tile([P, count * N], U32, name="w2_codes", align_bytes=64)
+            scales = coded.tile([P, count * N], U8, name="w2_scales", align_bytes=64)
+            nc.vector.quantize_mx(
+                out=codes[:].bitcast(FP8X4), scales=scales[:], in_=w_bf
+            )
+            acc = psum_y.tile([P, count * C], F32, name="acc_y")
+            for i, e in enumerate(experts):
                 nc.tensor.matmul_mx(
-                    out=acc[:],
-                    lhsT=codes[:].bitcast(FP8X4),
-                    lhsT_scale=scales[:],
+                    out=acc[:, i * C : (i + 1) * C],
+                    lhsT=codes[:, i * N : (i + 1) * N].bitcast(FP8X4),
+                    lhsT_scale=scales[:, i * N : (i + 1) * N],
                     rhs=h_codes[e][:].bitcast(FP8X4),
                     rhs_scale=h_scales[e][:],
                     start=True,
                     stop=True,
                 )
-                nc.scalar.copy(out=y[:, e * C : (e + 1) * C], in_=acc[:])
+            nc.scalar.copy(out=y[:, experts[0] * C : (experts[-1] + 1) * C], in_=acc[:])
 
         back_lists = []
         for e in range(E):
@@ -144,14 +152,18 @@ def tile_moe_ecr_mlp_silu_kernel(
             first_layer(e)
             for experts in EARLY_W2:
                 if experts[-1] == e:
-                    second_layer(experts, load_w2(experts), nc.scalar.copy)
+                    early_bf = rounded.tile([P, len(experts) * H], BF16, name="w2_bf", align_bytes=64)
+                    second_layer(experts, early_bf[:], nc.scalar.copy)
             if e == 2:
                 for r, pos in enumerate((pos1, pos2, pos3, pos4)):
                     back = lists.tile([P, T // LIST_ROWS], U16, name="back%d" % r)
                     nc.sync.dma_start(back[:], pos)
                     back_lists.append(back)
-        for n, experts in enumerate(LATE_W2):
-            second_layer(experts, load_w2(experts), nc.scalar.copy if n == 0 else nc.vector.tensor_copy)
+        before_last, last_bf = w1_rounded[E - 1, PASSES - 2], w1_rounded[E - 1, PASSES - 1]
+        second_layer((2, 3), before_last[:, : 2 * H], nc.scalar.copy)
+        second_layer((4, 5), last_bf[:, 2 * H :], nc.vector.tensor_copy)
+        second_layer((6,), last_bf[:, :H], nc.vector.tensor_copy)
+        second_layer((7,), last_bf[:, H : 2 * H], nc.vector.tensor_copy)
 
         gates = []
         for r in range(TOP):

@@ -1,6 +1,7 @@
 from contextlib import ExitStack
 
 import concourse.mybir as mybir
+from concourse.masks import make_identity
 
 K, T, E, C, H, N = 1536, 768, 8, 128, 512, 128
 TOP = 4
@@ -23,13 +24,13 @@ P = 128
 PACK = 4
 PASSES = K // (P * PACK)
 LIST_ROWS = 16
-GATHER = 256
-STREAM_BUFS = 12
-VECTOR_M = 60
+GATHER = 512
+STREAM_BUFS = 4
+W1_LOADS = ((3,), (3,), (3,), (3,), (3,), (3,), (2, 1), (1, 1, 1))
+VECTOR_M = 72
 LAST_VECTOR_M = 84
-EARLY_W2 = ((0, 1),)
-TOKEN_CUTS = (0, 512, 640, 768)
-TAIL = [(w[0], int(w[1]), int(w[2])) for w in "g00 g01 g02 a01 g03 a02 g10 a03 g20 g11 g21 g12 a11 g22 a21 g13 a12 g23 a22 a13 a23".split()]
+EARLY_W2 = 2
+TOKEN_CUTS = (0, 384, 640, 768)
 
 
 def tile_moe_ecr_mlp_silu_kernel(
@@ -39,156 +40,263 @@ def tile_moe_ecr_mlp_silu_kernel(
     with ExitStack() as ctx:
         lists = ctx.enter_context(tc.tile_pool(name="lists", bufs=1))
         keep = ctx.enter_context(tc.tile_pool(name="keep", bufs=1))
-        stream = ctx.enter_context(tc.tile_pool(name="stream", bufs=STREAM_BUFS))
         rounded = ctx.enter_context(tc.tile_pool(name="rounded", bufs=4))
-        coded = ctx.enter_context(tc.tile_pool(name="coded", bufs=12))
+        coded = ctx.enter_context(tc.tile_pool(name="coded", bufs=6))
         slots_pool = ctx.enter_context(tc.tile_pool(name="slots", bufs=2))
-        psum_a = ctx.enter_context(tc.psum_pool(name="psum_a", bufs=3))
-        psum_y = ctx.enter_context(tc.psum_pool(name="psum_y", bufs=4))
+        psum_a = ctx.enter_context(tc.psum_pool(name="psum_a", bufs=2))
+        psum_y = ctx.enter_context(tc.psum_pool(name="psum_y", bufs=3))
+        psum_t = ctx.enter_context(tc.psum_pool(name="psum_t", bufs=2))
+        psum_s = ctx.enter_context(tc.psum_pool(name="psum_s", bufs=1))
 
         token_scales = keep.tile([P, T], U8, name="token_scales", align_bytes=64)
         nc.vector.memset(token_scales[:].bitcast(I32), 0)
-        for quad in range(4):
-            nc.scalar.dma_start(
-                out=token_scales[32 * quad : 32 * quad + 4 * PASSES, :].bitcast(I32),
-                in_=x_scales[:, 4 * quad : 4 * quad + 4, :].bitcast(I32),
-            )
-
         token_words = keep.tile([P, PASSES, T], I32, name="token_words", align_bytes=64)
         nc.sync.dma_start(out=token_words[:], in_=x_words.rearrange("o p t r -> p o (t r)").bitcast(I32))
         slot_list = lists.tile([P, SLOTS // LIST_ROWS], U16, name="slot_list")
         nc.sync.dma_start(slot_list[:], offs)
 
+        def load_scales():
+            staged = keep.tile([P, T // 4], I32, name="staged_scales")
+            for quad in range(4):
+                rows = slice(32 * quad, 32 * quad + 4 * PASSES)
+                nc.sync.dma_start(out=staged[rows, :], in_=x_scales[:, 4 * quad : 4 * quad + 4, :].bitcast(I32))
+            return staged
+
+        def place_scales(staged):
+            for quad in range(4):
+                rows = slice(32 * quad, 32 * quad + 4 * PASSES)
+                nc.vector.tensor_copy(out=token_scales[rows, :].bitcast(I32), in_=staged[rows, :])
+
         y = keep.tile([P, SLOTS + PAD], F32, name="y", align_bytes=64)
         nc.vector.memset(y[:, SLOTS:], 0.0)
 
-        slot_words, slot_scales, h_codes, h_scales, w1_rounded = {}, {}, {}, {}, {}
+        identity = keep.tile([P, P], F32, name="identity")
+        make_identity(nc, identity[:])
 
-        def gather_tokens(g):
+        gate_all = keep.tile([P, TOP * T], F32, name="gate_all")
+        gates = [gate_all[:, r * T : (r + 1) * T] for r in range(TOP)]
+
+        halves, blocks = 2, T // (2 * P)
+        staged_gate = keep.tile([TOP * halves, blocks * P], F32, name="staged_gate")
+        nc.sync.dma_start(out=staged_gate[:], in_=gate[:, 0, :].rearrange("r (h m) -> r h m", h=halves))
+
+        def spread_gate():
+            gate_rows = keep.tile([P, blocks * P], F32, name="gate_rows")
+            nc.gpsimd.memset(gate_rows[:], 0.0)
+            nc.gpsimd.tensor_copy(out=gate_rows[: TOP * halves, :], in_=staged_gate[:])
+            gate_turned = psum_t.tile([P, blocks, P], F32, name="gate_turned", tag="turn")
+            for b in range(blocks):
+                nc.tensor.transpose(gate_turned[:, b, :], gate_rows[:, b * P : (b + 1) * P], identity[:])
+            gate_cols = keep.tile([P, blocks, TOP * halves], F32, name="gate_cols")
+            nc.scalar.copy(out=gate_cols[:], in_=gate_turned[:, :, : TOP * halves])
+            for first in range(0, TOP * halves * blocks, 4):
+                spread = psum_t.tile([P, 4 * P], F32, name="spread", tag="turn")
+                for i in range(4):
+                    row, b = divmod(first + i, blocks)
+                    nc.tensor.transpose(
+                        spread[:, i * P : (i + 1) * P],
+                        gate_cols[:, b, row : row + 1].to_broadcast([P, P]),
+                        identity[:],
+                    )
+                nc.scalar.copy(out=gate_all[:, first * P : (first + 4) * P], in_=spread[:])
+
+        slot_words, slot_scales, h_codes, h_scales, w1_raw, sums = {}, {}, {}, {}, {}, {}
+
+        def gather_words(g):
             cols = slice(g * GATHER // LIST_ROWS, (g + 1) * GATHER // LIST_ROWS)
             words = slots_pool.tile([P, PASSES, GATHER], U32, name="slot_words", align_bytes=64)
-            scales = slots_pool.tile([P, GATHER], U8, name="slot_scales", align_bytes=64)
             for o in range(PASSES):
                 nc.vector.tensor_copy(words[:, o, :], token_words[:, o, :].bitcast(U32).indirect(slot_list[:, cols]))
-            nc.vector.tensor_copy(scales[:], token_scales[:].indirect(slot_list[:, cols]))
-            slot_words[g], slot_scales[g] = words, scales
+            slot_words[g] = words
 
-        def first_layer(e):
+        def gather_scales(g):
+            cols = slice(g * GATHER // LIST_ROWS, (g + 1) * GATHER // LIST_ROWS)
+            scales = slots_pool.tile([P, GATHER], U8, name="slot_scales", align_bytes=64)
+            nc.vector.tensor_copy(scales[:], token_scales[:].indirect(slot_list[:, cols]))
+            slot_scales[g] = scales
+
+        arena = [
+            keep.tile([P, PASSES * PACK * H], F32, name="arena%d" % i, align_bytes=64) for i in range(STREAM_BUFS)
+        ]
+
+        def load_w1(e, o0, count):
+            raw = arena[e % STREAM_BUFS][:, o0 * PACK * H : (o0 + count) * PACK * H]
+            rows = w1[e, o0 * P * PACK : (o0 + count) * P * PACK, :]
+            nc.sync.dma_start(
+                out=raw.rearrange("p (o x) -> p o x", o=count), in_=rows.rearrange("(o p j) c -> p o (j c)", p=P, j=PACK)
+            )
+            return raw
+
+        def first_layer(e, preloaded=None):
             g, first = divmod(e * C, GATHER)
             slots = slice(first, first + C)
             acc = psum_a.tile([P, PACK, C], F32, name="acc")
-            for o in range(PASSES):
-                raw = stream.tile([P, PACK, H], F32, name="raw", tag="stream")
-                nc.sync.dma_start(
-                    out=raw[:], in_=w1[e, o * P * PACK : (o + 1) * P * PACK, :].rearrange("(p j) c -> p j c", j=PACK)
-                )
-                w_bf = rounded.tile([P, H * PACK], BF16, name="w1_bf", align_bytes=64)
-                w1_rounded[e, o] = w_bf
-                dst = w_bf[:].rearrange("p (t m j) -> p m j t", t=PACK, j=PACK)
-                src = raw[:].rearrange("p j (m t) -> p m j t", t=PACK)
-                last = e == E - 1 and o == PASSES - 1
-                split = LAST_VECTOR_M if last else VECTOR_M
-                nc.vector.tensor_copy(out=dst[:, :split], in_=src[:, :split])
-                nc.scalar.copy(out=dst[:, split:], in_=src[:, split:])
-                codes = coded.tile([P, H], U32, name="w1_codes", align_bytes=64)
-                scales = coded.tile([P, H], U8, name="w1_scales", align_bytes=64)
-                width = H // 2 if last else H
-                for c0 in range(0, H, width):
-                    nc.vector.quantize_mx(
-                        out=codes[:, c0 : c0 + width].bitcast(FP8X4),
-                        scales=scales[:, c0 : c0 + width],
-                        in_=w_bf[:, c0 * PACK : (c0 + width) * PACK],
+            o0 = 0
+            for count in W1_LOADS[e]:
+                raw = preloaded if preloaded is not None else load_w1(e, o0, count)
+                w1_raw[e, o0] = raw
+                for o in range(o0, o0 + count):
+                    if e < E - 1 or o < PASSES - 1:
+                        w_bf = rounded.tile([P, H * PACK], BF16, name="w1_bf", align_bytes=64)
+                    dst = w_bf[:].rearrange("p (t m j) -> p m j t", t=PACK, j=PACK)
+                    src = raw[:, (o - o0) * PACK * H : (o - o0 + 1) * PACK * H].rearrange(
+                        "p (j m t) -> p m j t", j=PACK, t=PACK
                     )
-                for t in range(PACK):
-                    cols = slice(t * P, (t + 1) * P)
-                    nc.tensor.matmul_mx(
-                        out=acc[:, t, :],
-                        lhsT=codes[:, cols].bitcast(FP8X4),
-                        lhsT_scale=scales[:, cols],
-                        rhs=slot_words[g][:, o, slots].bitcast(FP8X4),
-                        rhs_scale=slot_scales[g][4 * o :, slots],
-                        start=(o == 0 and t == 0),
-                        stop=(o == PASSES - 1 and t == PACK - 1),
-                    )
-            h_bf = rounded.tile([P, C, PACK], BF16, name="h_bf", align_bytes=64)
-            nc.scalar.activation(out=h_bf[:], in_=acc[:].rearrange("p t s -> p s t"), func=SILU)
+                    last = e == E - 1 and o == PASSES - 1
+                    split = LAST_VECTOR_M if last else VECTOR_M
+                    nc.vector.tensor_copy(out=dst[:, :split], in_=src[:, :split])
+                    nc.scalar.copy(out=dst[:, split:], in_=src[:, split:])
+                    if o == 0 and e > 0:
+                        activate(e - 1, raw.bitcast(BF16)[:, H : 2 * H])
+                    codes = coded.tile([P, H], U32, name="w1_codes", align_bytes=64)
+                    scales = coded.tile([P, H], U8, name="w1_scales", align_bytes=64)
+                    width = H // 2 if last else H
+                    for c0 in range(0, H, width):
+                        nc.vector.quantize_mx(
+                            out=codes[:, c0 : c0 + width].bitcast(FP8X4),
+                            scales=scales[:, c0 : c0 + width],
+                            in_=w_bf[:, c0 * PACK : (c0 + width) * PACK],
+                        )
+                    for t in range(PACK):
+                        cols = slice(t * P, (t + 1) * P)
+                        nc.tensor.matmul_mx(
+                            out=acc[:, t, :],
+                            lhsT=codes[:, cols].bitcast(FP8X4),
+                            lhsT_scale=scales[:, cols],
+                            rhs=slot_words[g][:, o, slots].bitcast(FP8X4),
+                            rhs_scale=slot_scales[g][4 * o :, slots],
+                            start=(o == 0 and t == 0),
+                            stop=(o == PASSES - 1 and t == PACK - 1),
+                        )
+                o0 += count
+            sums[e] = acc
+
+        def activate(e, h_bf):
+            nc.scalar.activation(
+                out=h_bf.rearrange("p (s t) -> p s t", t=PACK), in_=sums[e][:].rearrange("p t s -> p s t"), func=SILU
+            )
             h_codes[e] = keep.tile([P, C], U32, name="h_codes%d" % e, align_bytes=64)
             h_scales[e] = keep.tile([P, C], U8, name="h_scales%d" % e, align_bytes=64)
             nc.vector.quantize_mx(
-                out=h_codes[e][:].bitcast(FP8X4), scales=h_scales[e][:], in_=h_bf[:].rearrange("p s t -> p (s t)")
+                out=h_codes[e][:].bitcast(FP8X4), scales=h_scales[e][:], in_=h_bf
             )
 
-        def second_layer(experts, w_bf, copy):
-            count = len(experts)
-            for i, e in enumerate(experts):
-                raw = stream.tile([P, PACK * N], F32, name="raw2", tag="stream")
-                nc.sync.dma_start(out=raw[:], in_=w2[e].rearrange("(p j) n -> p (j n)", j=PACK))
-                copy(
-                    out=w_bf[:, i * H : (i + 1) * H].rearrange("p (c i j) -> p c j i", i=4, j=PACK),
-                    in_=raw[:].rearrange("p (j c i) -> p c j i", i=4, j=PACK),
-                )
+        def load_w2(first, count, raw):
+            nc.sync.dma_start(
+                out=raw.rearrange("p (e x) -> p e x", e=count),
+                in_=w2[first : first + count].rearrange("e (p j) n -> p e (j n)", j=PACK),
+            )
+            return raw
+
+        def round_w2(raw, w_bf, copy):
+            copy(
+                out=w_bf.rearrange("p (e c i j) -> p e c j i", c=N // 4, i=4, j=PACK),
+                in_=raw.rearrange("p (e j c i) -> p e c j i", c=N // 4, i=4, j=PACK),
+            )
+
+        def second_layer(first, count, w_bf):
             codes = coded.tile([P, count * N], U32, name="w2_codes", align_bytes=64)
             scales = coded.tile([P, count * N], U8, name="w2_scales", align_bytes=64)
-            nc.vector.quantize_mx(
-                out=codes[:].bitcast(FP8X4), scales=scales[:], in_=w_bf
-            )
+            nc.vector.quantize_mx(out=codes[:].bitcast(FP8X4), scales=scales[:], in_=w_bf)
             acc = psum_y.tile([P, count * C], F32, name="acc_y")
-            for i, e in enumerate(experts):
+            for i in range(count):
                 nc.tensor.matmul_mx(
                     out=acc[:, i * C : (i + 1) * C],
                     lhsT=codes[:, i * N : (i + 1) * N].bitcast(FP8X4),
                     lhsT_scale=scales[:, i * N : (i + 1) * N],
-                    rhs=h_codes[e][:].bitcast(FP8X4),
-                    rhs_scale=h_scales[e][:],
+                    rhs=h_codes[first + i][:].bitcast(FP8X4),
+                    rhs_scale=h_scales[first + i][:],
                     start=True,
                     stop=True,
                 )
-            nc.scalar.copy(out=y[:, experts[0] * C : (experts[-1] + 1) * C], in_=acc[:])
+            return acc
 
+        def put_results(first, count, acc):
+            nc.scalar.copy(out=y[:, first * C : (first + count) * C], in_=acc[:])
+
+        first_raw = load_w1(0, 0, PASSES)
+        staged_scales = load_scales()
+        spread_gate()
+        for g in range(SLOTS // GATHER):
+            gather_words(g)
+        place_scales(staged_scales)
+        for g in range(SLOTS // GATHER):
+            gather_scales(g)
         back_lists = []
         for e in range(E):
-            if (e * C) % GATHER == 0:
-                gather_tokens(e * C // GATHER)
-            first_layer(e)
-            for experts in EARLY_W2:
-                if experts[-1] == e:
-                    early_bf = rounded.tile([P, len(experts) * H], BF16, name="w2_bf", align_bytes=64)
-                    second_layer(experts, early_bf[:], nc.scalar.copy)
+            first_layer(e, first_raw if e == 0 else None)
+            if e == EARLY_W2:
+                early_raw = keep.tile([P, EARLY_W2 * H], F32, name="early_raw")
+                early_bf = keep.tile([P, EARLY_W2 * H], BF16, name="w2_bf", align_bytes=64)
+                round_w2(load_w2(0, EARLY_W2, early_raw[:]), early_bf[:], nc.scalar.copy)
+                put_results(0, EARLY_W2, second_layer(0, EARLY_W2, early_bf[:]))
             if e == 2:
                 for r, pos in enumerate((pos1, pos2, pos3, pos4)):
                     back = lists.tile([P, T // LIST_ROWS], U16, name="back%d" % r)
                     nc.sync.dma_start(back[:], pos)
                     back_lists.append(back)
-        before_last, last_bf = w1_rounded[E - 1, PASSES - 2], w1_rounded[E - 1, PASSES - 1]
-        second_layer((2, 3), before_last[:, : 2 * H], nc.scalar.copy)
-        second_layer((4, 5), last_bf[:, 2 * H :], nc.vector.tensor_copy)
-        second_layer((6,), last_bf[:, :H], nc.vector.tensor_copy)
-        second_layer((7,), last_bf[:, H : 2 * H], nc.vector.tensor_copy)
+        last_h = keep.tile([P, H], BF16, name="last_h", align_bytes=64)
+        activate(E - 1, last_h[:])
+        late_bf = w1_raw[E - 1, PASSES - 1].bitcast(BF16)
 
-        gates = []
-        for r in range(TOP):
-            g_tile = stream.tile([P, T], F32, name="gate", tag="stream")
-            nc.sync.dma_start(out=g_tile[:], in_=gate[r])
-            gates.append(g_tile)
+        def late(first, count, place):
+            return load_w2(first, count, arena[0][:, place * H : (place + count) * H])
 
-        chunks = [(lo, hi) for lo, hi in zip(TOKEN_CUTS[:-1], TOKEN_CUTS[1:])]
-        parts, sums = {}, {}
+        round_w2(late(6, 2, 0), late_bf[:, : 2 * H], nc.scalar.copy)
+        round_w2(late(2, 1, 2), late_bf[:, 2 * H : 3 * H], nc.vector.tensor_copy)
+        round_w2(late(3, 1, 3), late_bf[:, 3 * H : 4 * H], nc.vector.tensor_copy)
+        acc67 = second_layer(6, 2, late_bf[:, : 2 * H])
+        acc23 = second_layer(2, 2, late_bf[:, 2 * H : 4 * H])
+        round_w2(late(4, 1, 4), late_bf[:, :H], nc.scalar.copy)
+        round_w2(late(5, 1, 5), late_bf[:, H : 2 * H], nc.vector.tensor_copy)
+        put_results(2, 2, acc23)
+        put_results(6, 2, acc67)
+        put_results(4, 1, second_layer(4, 1, late_bf[:, :H]))
+        put_results(5, 1, second_layer(5, 1, late_bf[:, H : 2 * H]))
 
-        def fetch(c, r):
-            lo, hi = chunks[c]
-            part = keep.tile([P, hi - lo], F32, name="part%d_%d" % (c, r))
+        def fetch(lo, hi, r):
+            part = keep.tile([P, hi - lo], F32, name="part%d_%d" % (lo, r))
             nc.vector.tensor_tensor(
                 part[:], y[:].indirect(back_lists[r][:, lo // LIST_ROWS : hi // LIST_ROWS]), gates[r][:, lo:hi], MULT
             )
-            parts[c, r] = part
+            return part
 
-        def add(c, r):
-            lo, hi = chunks[c]
-            total = keep.tile([P, hi - lo], F32, name="sum%d_%d" % (c, r))
-            nc.vector.tensor_tensor(total[:], (parts[c, 0] if r == 1 else sums[c])[:], parts[c, r][:], ADD)
-            sums[c] = total
-            if r == TOP - 1:
-                (nc.sync if c % 2 == 0 else nc.scalar).dma_start(out=out[:, lo:hi], in_=total[:])
+        def combine_on_tensor(lo, hi):
+            blocks = [slice(b, b + P) for b in range(0, hi - lo, P)]
+            turned = psum_s.tile([P, hi - lo], F32, name="turned")
+            for r in range(TOP):
+                part = fetch(lo, hi, r)
+                for b, cols in enumerate(blocks):
+                    nc.tensor.matmul(
+                        turned[:, cols],
+                        lhsT=part[:, cols],
+                        rhs=identity[:],
+                        is_transpose=True,
+                        start=(r == 0 and b == 0),
+                        stop=(r == TOP - 1 and b == len(blocks) - 1),
+                    )
+            by_token = keep.tile([P, hi - lo], F32, name="by_token")
+            nc.scalar.copy(out=by_token[:], in_=turned[:])
+            upright = psum_t.tile([P, hi - lo], F32, name="upright", tag="turn")
+            for cols in blocks:
+                nc.tensor.transpose(upright[:, cols], by_token[:, cols], identity[:])
+            total = keep.tile([P, hi - lo], F32, name="total%d" % lo)
+            nc.scalar.copy(out=total[:], in_=upright[:])
+            nc.scalar.dma_start(out=out[:, lo:hi], in_=total[:])
 
-        for step, c, r in TAIL:
-            (fetch if step == "g" else add)(c, r)
+        def combine_on_vector(lo, hi):
+            def add(name, a, b):
+                total = keep.tile([P, hi - lo], F32, name=name)
+                nc.vector.tensor_tensor(total[:], a[:], b[:], ADD)
+                return total
+
+            p0, p1, p2 = fetch(lo, hi, 0), fetch(lo, hi, 1), fetch(lo, hi, 2)
+            s01 = add("s01", p0, p1)
+            p3 = fetch(lo, hi, 3)
+            s012 = add("s012", s01, p2)
+            total = add("s0123", s012, p3)
+            nc.sync.dma_start(out=out[:, lo:hi], in_=total[:])
+
+        combine_on_tensor(TOKEN_CUTS[0], TOKEN_CUTS[1])
+        combine_on_tensor(TOKEN_CUTS[1], TOKEN_CUTS[2])
+        combine_on_vector(TOKEN_CUTS[2], TOKEN_CUTS[3])

@@ -30,7 +30,7 @@ W1_LOADS = ((3,), (3,), (3,), (3,), (3,), (3,), (2, 1), (1, 1, 1))
 VECTOR_M = 72
 LAST_VECTOR_M = 84
 EARLY_W2 = 2
-TOKEN_CUTS = (0, 384, 640, 768)
+TOKEN_CUTS = (0, 256, 512, 768)
 
 
 def tile_moe_ecr_mlp_silu_kernel(

@@ -44,9 +44,8 @@ def tile_moe_ecr_mlp_silu_kernel(
         coded = ctx.enter_context(tc.tile_pool(name="coded", bufs=6))
         slots_pool = ctx.enter_context(tc.tile_pool(name="slots", bufs=2))
         psum_a = ctx.enter_context(tc.psum_pool(name="psum_a", bufs=2))
-        psum_y = ctx.enter_context(tc.psum_pool(name="psum_y", bufs=3))
+        psum_y = ctx.enter_context(tc.psum_pool(name="psum_y", bufs=4))
         psum_t = ctx.enter_context(tc.psum_pool(name="psum_t", bufs=2))
-        psum_s = ctx.enter_context(tc.psum_pool(name="psum_s", bufs=1))
 
         token_scales = keep.tile([P, T], U8, name="token_scales", align_bytes=64)
         nc.vector.memset(token_scales[:].bitcast(I32), 0)
@@ -130,7 +129,7 @@ def tile_moe_ecr_mlp_silu_kernel(
         def first_layer(e, preloaded=None):
             g, first = divmod(e * C, GATHER)
             slots = slice(first, first + C)
-            acc = psum_a.tile([P, PACK, C], F32, name="acc")
+            acc = psum_a.tile([P, PACK, C], F32, name="acc", tag="acc")
             o0 = 0
             for count in W1_LOADS[e]:
                 raw = preloaded if preloaded is not None else load_w1(e, o0, count)
@@ -263,7 +262,7 @@ def tile_moe_ecr_mlp_silu_kernel(
 
         def combine_on_tensor(lo, hi):
             blocks = [slice(b, b + P) for b in range(0, hi - lo, P)]
-            turned = psum_s.tile([P, hi - lo], F32, name="turned")
+            turned = psum_a.tile([P, hi - lo], F32, name="turned", tag="acc")
             for r in range(TOP):
                 part = fetch(lo, hi, r)
                 for b, cols in enumerate(blocks):
@@ -286,16 +285,19 @@ def tile_moe_ecr_mlp_silu_kernel(
 
         def combine_on_vector(lo, hi):
             def add(name, a, b):
-                total = keep.tile([P, hi - lo], F32, name=name)
-                nc.vector.tensor_tensor(total[:], a[:], b[:], ADD)
+                total = keep.tile([P, a.shape[1]], F32, name=name)
+                nc.vector.tensor_tensor(total[:], a, b, ADD)
                 return total
 
             p0, p1, p2 = fetch(lo, hi, 0), fetch(lo, hi, 1), fetch(lo, hi, 2)
-            s01 = add("s01", p0, p1)
+            s01 = add("s01", p0[:], p1[:])
             p3 = fetch(lo, hi, 3)
-            s012 = add("s012", s01, p2)
-            total = add("s0123", s012, p3)
-            nc.sync.dma_start(out=out[:, lo:hi], in_=total[:])
+            width = (hi - lo) // 2
+            halves_c = [slice(0, width), slice(width, 2 * width)]
+            s012 = [add("s012_%d" % i, s01[:, c], p2[:, c]) for i, c in enumerate(halves_c)]
+            for i, c in enumerate(halves_c):
+                total = add("s0123_%d" % i, s012[i][:], p3[:, c])
+                nc.sync.dma_start(out=out[:, lo + c.start : lo + c.stop], in_=total[:])
 
         combine_on_tensor(TOKEN_CUTS[0], TOKEN_CUTS[1])
         combine_on_tensor(TOKEN_CUTS[1], TOKEN_CUTS[2])

@@ -72,33 +72,6 @@ def tile_moe_ecr_mlp_silu_kernel(
         identity = keep.tile([P, P], F32, name="identity")
         make_identity(nc, identity[:])
 
-        gate_all = keep.tile([P, TOP * T], F32, name="gate_all")
-        gates = [gate_all[:, r * T : (r + 1) * T] for r in range(TOP)]
-
-        halves, blocks = 2, T // (2 * P)
-        staged_gate = keep.tile([TOP * halves, blocks * P], F32, name="staged_gate")
-        nc.sync.dma_start(out=staged_gate[:], in_=gate[:, 0, :].rearrange("r (h m) -> r h m", h=halves))
-
-        def spread_gate():
-            gate_rows = keep.tile([P, blocks * P], F32, name="gate_rows")
-            nc.gpsimd.memset(gate_rows[:], 0.0)
-            nc.gpsimd.tensor_copy(out=gate_rows[: TOP * halves, :], in_=staged_gate[:])
-            gate_turned = psum_t.tile([P, blocks, P], F32, name="gate_turned", tag="turn")
-            for b in range(blocks):
-                nc.tensor.transpose(gate_turned[:, b, :], gate_rows[:, b * P : (b + 1) * P], identity[:])
-            gate_cols = keep.tile([P, blocks, TOP * halves], F32, name="gate_cols")
-            nc.scalar.copy(out=gate_cols[:], in_=gate_turned[:, :, : TOP * halves])
-            for first in range(0, TOP * halves * blocks, 4):
-                spread = psum_t.tile([P, 4 * P], F32, name="spread", tag="turn")
-                for i in range(4):
-                    row, b = divmod(first + i, blocks)
-                    nc.tensor.transpose(
-                        spread[:, i * P : (i + 1) * P],
-                        gate_cols[:, b, row : row + 1].to_broadcast([P, P]),
-                        identity[:],
-                    )
-                nc.scalar.copy(out=gate_all[:, first * P : (first + 4) * P], in_=spread[:])
-
         slot_words, slot_scales, h_codes, h_scales, w1_raw, sums = {}, {}, {}, {}, {}, {}
 
         def gather_words(g):
@@ -215,7 +188,6 @@ def tile_moe_ecr_mlp_silu_kernel(
 
         first_raw = load_w1(0, 0, PASSES)
         staged_scales = load_scales()
-        spread_gate()
         for g in range(SLOTS // GATHER):
             gather_words(g)
         place_scales(staged_scales)
@@ -229,11 +201,6 @@ def tile_moe_ecr_mlp_silu_kernel(
                 early_bf = keep.tile([P, EARLY_W2 * H], BF16, name="w2_bf", align_bytes=64)
                 round_w2(load_w2(0, EARLY_W2, early_raw[:]), early_bf[:], nc.scalar.copy)
                 put_results(0, EARLY_W2, second_layer(0, EARLY_W2, early_bf[:]))
-            if e == 2:
-                for r, pos in enumerate((pos1, pos2, pos3, pos4)):
-                    back = lists.tile([P, T // LIST_ROWS], U16, name="back%d" % r)
-                    nc.sync.dma_start(back[:], pos)
-                    back_lists.append(back)
         last_h = keep.tile([P, H], BF16, name="last_h", align_bytes=64)
         activate(E - 1, last_h[:])
         late_bf = w1_raw[E - 1, PASSES - 1].bitcast(BF16)
@@ -253,10 +220,27 @@ def tile_moe_ecr_mlp_silu_kernel(
         put_results(4, 1, second_layer(4, 1, late_bf[:, :H]))
         put_results(5, 1, second_layer(5, 1, late_bf[:, H : 2 * H]))
 
+        gates = {}
+        for lo, hi in zip(TOKEN_CUTS, TOKEN_CUTS[1:]):
+            first = 6 * H + TOP * lo
+            gates[lo] = arena[0][:, first : first + TOP * (hi - lo)].rearrange("p (r t) -> p r t", r=TOP)
+
+        def load_gate(lo, hi, r0, r1):
+            nc.sync.dma_start(out=gates[lo][:, r0:r1, :], in_=gate[r0:r1, :, lo:hi].rearrange("r n t -> n r t"))
+
+        for r, pos in enumerate((pos1, pos2, pos3, pos4)):
+            back = lists.tile([P, T // LIST_ROWS], U16, name="back%d" % r)
+            nc.sync.dma_start(back[:], pos)
+            back_lists.append(back)
+            if r % 2 == 1:
+                load_gate(TOKEN_CUTS[0], TOKEN_CUTS[1], r - 1, r + 1)
+        for lo, hi in zip(TOKEN_CUTS[1:], TOKEN_CUTS[2:]):
+            load_gate(lo, hi, 0, TOP)
+
         def fetch(lo, hi, r):
             part = keep.tile([P, hi - lo], F32, name="part%d_%d" % (lo, r))
             nc.vector.tensor_tensor(
-                part[:], y[:].indirect(back_lists[r][:, lo // LIST_ROWS : hi // LIST_ROWS]), gates[r][:, lo:hi], MULT
+                part[:], y[:].indirect(back_lists[r][:, lo // LIST_ROWS : hi // LIST_ROWS]), gates[lo][:, r, :], MULT
             )
             return part
 

@@ -24,12 +24,14 @@ P = 128
 PACK = 4
 PASSES = K // (P * PACK)
 LIST_ROWS = 16
-GATHER = 512
+WINDOW = 1408
 STREAM_BUFS = 4
+PASS_BYTES = PACK * H * 4
+SLOT_BYTES = PASSES * PASS_BYTES
 W1_LOADS = ((3,), (3,), (3,), (3,), (3,), (3,), (2, 1), (1, 1, 1))
 VECTOR_M = 72
 LAST_VECTOR_M = 84
-EARLY_W2 = 2
+EARLY_AT = 2
 TOKEN_CUTS = (0, 256, 512, 768)
 
 
@@ -40,17 +42,18 @@ def tile_moe_ecr_mlp_silu_kernel(
     with ExitStack() as ctx:
         lists = ctx.enter_context(tc.tile_pool(name="lists", bufs=1))
         keep = ctx.enter_context(tc.tile_pool(name="keep", bufs=1))
+        ring = ctx.enter_context(tc.tile_pool(name="ring", bufs=1))
         rounded = ctx.enter_context(tc.tile_pool(name="rounded", bufs=4))
         coded = ctx.enter_context(tc.tile_pool(name="coded", bufs=6))
-        slots_pool = ctx.enter_context(tc.tile_pool(name="slots", bufs=2))
         psum_a = ctx.enter_context(tc.psum_pool(name="psum_a", bufs=2))
         psum_y = ctx.enter_context(tc.psum_pool(name="psum_y", bufs=4))
         psum_t = ctx.enter_context(tc.psum_pool(name="psum_t", bufs=2))
 
-        token_scales = keep.tile([P, T], U8, name="token_scales", align_bytes=64)
+        token_scales = keep.tile([P, WINDOW], U8, name="token_scales", align_bytes=64)
         nc.vector.memset(token_scales[:].bitcast(I32), 0)
-        token_words = keep.tile([P, PASSES, T], I32, name="token_words", align_bytes=64)
-        nc.sync.dma_start(out=token_words[:], in_=x_words.rearrange("o p t r -> p o (t r)").bitcast(I32))
+        token_words = keep.tile([P, (PASSES - 1) * T + WINDOW], I32, name="token_words", align_bytes=64)
+        nc.vector.memset(token_words[:, PASSES * T :], 0)
+        nc.sync.dma_start(out=token_words[:, : PASSES * T].rearrange("p (o t) -> p o t", o=PASSES), in_=x_words.rearrange("o p t r -> p o (t r)").bitcast(I32))
         slot_list = lists.tile([P, SLOTS // LIST_ROWS], U16, name="slot_list")
         nc.sync.dma_start(slot_list[:], offs)
 
@@ -64,7 +67,7 @@ def tile_moe_ecr_mlp_silu_kernel(
         def place_scales(staged):
             for quad in range(4):
                 rows = slice(32 * quad, 32 * quad + 4 * PASSES)
-                nc.vector.tensor_copy(out=token_scales[rows, :].bitcast(I32), in_=staged[rows, :])
+                nc.vector.tensor_copy(out=token_scales[rows, :T].bitcast(I32), in_=staged[rows, :])
 
         y = keep.tile([P, SLOTS + PAD], F32, name="y", align_bytes=64)
         nc.vector.memset(y[:, SLOTS:], 0.0)
@@ -72,27 +75,51 @@ def tile_moe_ecr_mlp_silu_kernel(
         identity = keep.tile([P, P], F32, name="identity")
         make_identity(nc, identity[:])
 
-        slot_words, slot_scales, h_codes, h_scales, w1_raw, sums = {}, {}, {}, {}, {}, {}
+        gate_all = keep.tile([P, TOP * T], F32, name="gate_all")
+        gates = [gate_all[:, r * T : (r + 1) * T] for r in range(TOP)]
 
-        def gather_words(g):
-            cols = slice(g * GATHER // LIST_ROWS, (g + 1) * GATHER // LIST_ROWS)
-            words = slots_pool.tile([P, PASSES, GATHER], U32, name="slot_words", align_bytes=64)
+        halves, blocks = 2, T // (2 * P)
+        staged_gate = keep.tile([TOP * halves, blocks * P], F32, name="staged_gate")
+        nc.sync.dma_start(out=staged_gate[:], in_=gate[:, 0, :].rearrange("r (h m) -> r h m", h=halves))
+
+        def spread_gate():
+            gate_rows = keep.tile([P, blocks * P], F32, name="gate_rows")
+            nc.gpsimd.memset(gate_rows[:], 0.0)
+            nc.gpsimd.tensor_copy(out=gate_rows[: TOP * halves, :], in_=staged_gate[:])
+            gate_turned = psum_t.tile([P, blocks, P], F32, name="gate_turned", tag="turn")
+            for b in range(blocks):
+                nc.tensor.transpose(gate_turned[:, b, :], gate_rows[:, b * P : (b + 1) * P], identity[:])
+            gate_cols = keep.tile([P, blocks, TOP * halves], F32, name="gate_cols")
+            nc.scalar.copy(out=gate_cols[:], in_=gate_turned[:, :, : TOP * halves])
+            for first in range(0, TOP * halves * blocks, 4):
+                spread = psum_t.tile([P, 4 * P], F32, name="spread", tag="turn")
+                for i in range(4):
+                    row, b = divmod(first + i, blocks)
+                    nc.tensor.transpose(
+                        spread[:, i * P : (i + 1) * P],
+                        gate_cols[:, b, row : row + 1].to_broadcast([P, P]),
+                        identity[:],
+                    )
+                nc.scalar.copy(out=gate_all[:, first * P : (first + 4) * P], in_=spread[:])
+
+        h_codes, h_scales, sums = {}, {}, {}
+
+        slot_words = keep.tile([P, PASSES, SLOTS], U32, name="slot_words", align_bytes=64)
+        slot_scales = keep.tile([P, SLOTS], U8, name="slot_scales", align_bytes=64)
+
+        def gather_words():
             for o in range(PASSES):
-                nc.vector.tensor_copy(words[:, o, :], token_words[:, o, :].bitcast(U32).indirect(slot_list[:, cols]))
-            slot_words[g] = words
+                window = token_words[:, o * T : o * T + WINDOW].bitcast(U32)
+                nc.vector.tensor_copy(slot_words[:, o, :], window.indirect(slot_list[:]))
 
-        def gather_scales(g):
-            cols = slice(g * GATHER // LIST_ROWS, (g + 1) * GATHER // LIST_ROWS)
-            scales = slots_pool.tile([P, GATHER], U8, name="slot_scales", align_bytes=64)
-            nc.vector.tensor_copy(scales[:], token_scales[:].indirect(slot_list[:, cols]))
-            slot_scales[g] = scales
+        def gather_scales():
+            nc.vector.tensor_copy(slot_scales[:], token_scales[:].indirect(slot_list[:]))
 
-        arena = [
-            keep.tile([P, PASSES * PACK * H], F32, name="arena%d" % i, align_bytes=64) for i in range(STREAM_BUFS)
-        ]
+        def ring_tile(name, columns, dtype, slot, byte):
+            return ring.tile([P, columns], dtype, name=name, align_bytes=64, offset=slot * SLOT_BYTES + byte)[:]
 
         def load_w1(e, o0, count):
-            raw = arena[e % STREAM_BUFS][:, o0 * PACK * H : (o0 + count) * PACK * H]
+            raw = ring_tile("raw%d_%d" % (e, o0), count * PACK * H, F32, e % STREAM_BUFS, o0 * PASS_BYTES)
             rows = w1[e, o0 * P * PACK : (o0 + count) * P * PACK, :]
             nc.sync.dma_start(
                 out=raw.rearrange("p (o x) -> p o x", o=count), in_=rows.rearrange("(o p j) c -> p o (j c)", p=P, j=PACK)
@@ -100,46 +127,48 @@ def tile_moe_ecr_mlp_silu_kernel(
             return raw
 
         def first_layer(e, preloaded=None):
-            g, first = divmod(e * C, GATHER)
-            slots = slice(first, first + C)
+            slots = slice(e * C, (e + 1) * C)
             acc = psum_a.tile([P, PACK, C], F32, name="acc", tag="acc")
             o0 = 0
             for count in W1_LOADS[e]:
                 raw = preloaded if preloaded is not None else load_w1(e, o0, count)
-                w1_raw[e, o0] = raw
-                for o in range(o0, o0 + count):
-                    if e < E - 1 or o < PASSES - 1:
-                        w_bf = rounded.tile([P, H * PACK], BF16, name="w1_bf", align_bytes=64)
-                    dst = w_bf[:].rearrange("p (t m j) -> p m j t", t=PACK, j=PACK)
-                    src = raw[:, (o - o0) * PACK * H : (o - o0 + 1) * PACK * H].rearrange(
-                        "p (j m t) -> p m j t", j=PACK, t=PACK
+                steps = [(o0, count)] if count == PASSES else [(o, 1) for o in range(o0, o0 + count)]
+                for s0, n in steps:
+                    last = e == E - 1 and s0 == PASSES - 1
+                    if not last:
+                        w_bf = rounded.tile(
+                            [P, n * H * PACK], BF16, name="w1_bf%d" % n, align_bytes=64, bufs=2 if n > 1 else 4
+                        )
+                    dst = w_bf[:].rearrange("p (o t m j) -> p o m j t", o=n, t=PACK, j=PACK)
+                    src = raw[:, (s0 - o0) * PACK * H : (s0 - o0 + n) * PACK * H].rearrange(
+                        "p (o j m t) -> p o m j t", o=n, j=PACK, t=PACK
                     )
-                    last = e == E - 1 and o == PASSES - 1
                     split = LAST_VECTOR_M if last else VECTOR_M
-                    nc.vector.tensor_copy(out=dst[:, :split], in_=src[:, :split])
-                    nc.scalar.copy(out=dst[:, split:], in_=src[:, split:])
-                    if o == 0 and e > 0:
-                        activate(e - 1, raw.bitcast(BF16)[:, H : 2 * H])
-                    codes = coded.tile([P, H], U32, name="w1_codes", align_bytes=64)
-                    scales = coded.tile([P, H], U8, name="w1_scales", align_bytes=64)
-                    width = H // 2 if last else H
-                    for c0 in range(0, H, width):
+                    nc.vector.tensor_copy(out=dst[:, :, :split], in_=src[:, :, :split])
+                    nc.scalar.copy(out=dst[:, :, split:], in_=src[:, :, split:])
+                    codes = coded.tile([P, n * H], U32, name="w1_codes%d" % n, align_bytes=64, bufs=2 if n > 1 else 4)
+                    scales = coded.tile([P, n * H], U8, name="w1_scales%d" % n, align_bytes=64, bufs=2 if n > 1 else 4)
+                    cuts = (0, H // 2, H) if last else (0, 2 * H, 3 * H) if n > 1 else (0, H)
+                    for c0, c1 in zip(cuts, cuts[1:]):
                         nc.vector.quantize_mx(
-                            out=codes[:, c0 : c0 + width].bitcast(FP8X4),
-                            scales=scales[:, c0 : c0 + width],
-                            in_=w_bf[:, c0 * PACK : (c0 + width) * PACK],
+                            out=codes[:, c0:c1].bitcast(FP8X4),
+                            scales=scales[:, c0:c1],
+                            in_=w_bf[:, c0 * PACK : c1 * PACK],
                         )
-                    for t in range(PACK):
-                        cols = slice(t * P, (t + 1) * P)
-                        nc.tensor.matmul_mx(
-                            out=acc[:, t, :],
-                            lhsT=codes[:, cols].bitcast(FP8X4),
-                            lhsT_scale=scales[:, cols],
-                            rhs=slot_words[g][:, o, slots].bitcast(FP8X4),
-                            rhs_scale=slot_scales[g][4 * o :, slots],
-                            start=(o == 0 and t == 0),
-                            stop=(o == PASSES - 1 and t == PACK - 1),
-                        )
+                    for o in range(s0, s0 + n):
+                        for t in range(PACK):
+                            cols = slice((o - s0) * H + t * P, (o - s0) * H + (t + 1) * P)
+                            nc.tensor.matmul_mx(
+                                out=acc[:, t, :],
+                                lhsT=codes[:, cols].bitcast(FP8X4),
+                                lhsT_scale=scales[:, cols],
+                                rhs=slot_words[:, o, slots].bitcast(FP8X4),
+                                rhs_scale=slot_scales[4 * o :, slots],
+                                start=(o == 0 and t == 0),
+                                stop=(o == PASSES - 1 and t == PACK - 1),
+                            )
+                if o0 == 0 and e > 0:
+                    activate(e - 1, ring_tile("h%d" % (e - 1), H, BF16, e % STREAM_BUFS, 0))
                 o0 += count
             sums[e] = acc
 
@@ -153,10 +182,10 @@ def tile_moe_ecr_mlp_silu_kernel(
                 out=h_codes[e][:].bitcast(FP8X4), scales=h_scales[e][:], in_=h_bf
             )
 
-        def load_w2(first, count, raw):
+        def load_w2(experts, raw):
             nc.sync.dma_start(
-                out=raw.rearrange("p (e x) -> p e x", e=count),
-                in_=w2[first : first + count].rearrange("e (p j) n -> p e (j n)", j=PACK),
+                out=raw.rearrange("p (e x) -> p e x", x=H),
+                in_=w2[experts].rearrange("e (p j) n -> p e (j n)", j=PACK),
             )
             return raw
 
@@ -166,18 +195,26 @@ def tile_moe_ecr_mlp_silu_kernel(
                 in_=raw.rearrange("p (e j c i) -> p e c j i", c=N // 4, i=4, j=PACK),
             )
 
-        def second_layer(first, count, w_bf):
-            codes = coded.tile([P, count * N], U32, name="w2_codes", align_bytes=64)
-            scales = coded.tile([P, count * N], U8, name="w2_scales", align_bytes=64)
+        w2_codes, w2_scales = {}, {}
+
+        def quantise_w2(experts, w_bf):
+            first, count = experts[0], len(experts)
+            codes = keep.tile([P, count * N], U32, name="w2_codes%d" % first, align_bytes=64)
+            scales = keep.tile([P, count * N], U8, name="w2_scales%d" % first, align_bytes=64)
             nc.vector.quantize_mx(out=codes[:].bitcast(FP8X4), scales=scales[:], in_=w_bf)
-            acc = psum_y.tile([P, count * C], F32, name="acc_y")
-            for i in range(count):
+            for i, e in enumerate(experts):
+                w2_codes[e] = codes[:, i * N : (i + 1) * N]
+                w2_scales[e] = scales[:, i * N : (i + 1) * N]
+
+        def second_layer(experts):
+            acc = psum_y.tile([P, len(experts) * C], F32, name="acc_y")
+            for i, e in enumerate(experts):
                 nc.tensor.matmul_mx(
                     out=acc[:, i * C : (i + 1) * C],
-                    lhsT=codes[:, i * N : (i + 1) * N].bitcast(FP8X4),
-                    lhsT_scale=scales[:, i * N : (i + 1) * N],
-                    rhs=h_codes[first + i][:].bitcast(FP8X4),
-                    rhs_scale=h_scales[first + i][:],
+                    lhsT=w2_codes[e].bitcast(FP8X4),
+                    lhsT_scale=w2_scales[e],
+                    rhs=h_codes[e][:].bitcast(FP8X4),
+                    rhs_scale=h_scales[e][:],
                     start=True,
                     stop=True,
                 )
@@ -188,59 +225,54 @@ def tile_moe_ecr_mlp_silu_kernel(
 
         first_raw = load_w1(0, 0, PASSES)
         staged_scales = load_scales()
-        for g in range(SLOTS // GATHER):
-            gather_words(g)
+        spread_gate()
+        gather_words()
         place_scales(staged_scales)
-        for g in range(SLOTS // GATHER):
-            gather_scales(g)
+        gather_scales()
         back_lists = []
         for e in range(E):
             first_layer(e, first_raw if e == 0 else None)
-            if e == EARLY_W2:
-                early_raw = keep.tile([P, EARLY_W2 * H], F32, name="early_raw")
-                early_bf = keep.tile([P, EARLY_W2 * H], BF16, name="w2_bf", align_bytes=64)
-                round_w2(load_w2(0, EARLY_W2, early_raw[:]), early_bf[:], nc.scalar.copy)
-                put_results(0, EARLY_W2, second_layer(0, EARLY_W2, early_bf[:]))
+            if e == EARLY_AT:
+                early_raw = keep.tile([P, 2 * H], F32, name="early_raw")
+                early_bf = keep.tile([P, 2 * H], BF16, name="w2_bf", align_bytes=64)
+                round_w2(load_w2(slice(0, 2), early_raw[:]), early_bf[:], nc.scalar.copy)
+                quantise_w2((0, 1), early_bf[:])
+                put_results(0, 2, second_layer((0, 1)))
         last_h = keep.tile([P, H], BF16, name="last_h", align_bytes=64)
         activate(E - 1, last_h[:])
-        late_bf = w1_raw[E - 1, PASSES - 1].bitcast(BF16)
 
         def late(first, count, place):
-            return load_w2(first, count, arena[0][:, place * H : (place + count) * H])
+            return load_w2(slice(first, first + count), ring_tile("w2_raw%d" % first, count * H, F32, 0, place * H * 4))
 
-        round_w2(late(6, 2, 0), late_bf[:, : 2 * H], nc.scalar.copy)
-        round_w2(late(2, 1, 2), late_bf[:, 2 * H : 3 * H], nc.vector.tensor_copy)
-        round_w2(late(3, 1, 3), late_bf[:, 3 * H : 4 * H], nc.vector.tensor_copy)
-        acc67 = second_layer(6, 2, late_bf[:, : 2 * H])
-        acc23 = second_layer(2, 2, late_bf[:, 2 * H : 4 * H])
-        round_w2(late(4, 1, 4), late_bf[:, :H], nc.scalar.copy)
-        round_w2(late(5, 1, 5), late_bf[:, H : 2 * H], nc.vector.tensor_copy)
-        put_results(2, 2, acc23)
-        put_results(6, 2, acc67)
-        put_results(4, 1, second_layer(4, 1, late_bf[:, :H]))
-        put_results(5, 1, second_layer(5, 1, late_bf[:, H : 2 * H]))
+        def late_bf(first, count, place):
+            byte = (PASSES - 1) * PASS_BYTES + place * H * 2
+            return ring_tile("w2_bf%d" % first, count * H, BF16, (E - 1) % STREAM_BUFS, byte)
 
-        gates = {}
-        for lo, hi in zip(TOKEN_CUTS, TOKEN_CUTS[1:]):
-            first = 6 * H + TOP * lo
-            gates[lo] = arena[0][:, first : first + TOP * (hi - lo)].rearrange("p (r t) -> p r t", r=TOP)
-
-        def load_gate(lo, hi, r0, r1):
-            nc.sync.dma_start(out=gates[lo][:, r0:r1, :], in_=gate[r0:r1, :, lo:hi].rearrange("r n t -> n r t"))
-
+        bf67, bf23 = late_bf(6, 2, 0), late_bf(2, 2, 2)
+        round_w2(late(6, 2, 0), bf67, nc.scalar.copy)
+        round_w2(late(2, 1, 2), bf23[:, :H], nc.vector.tensor_copy)
+        round_w2(late(3, 1, 3), bf23[:, H:], nc.vector.tensor_copy)
+        quantise_w2((6, 7), bf67)
+        acc67 = second_layer((6, 7))
+        quantise_w2((2, 3), bf23)
+        acc23 = second_layer((2, 3))
+        bf4, bf5 = late_bf(4, 1, 0), late_bf(5, 1, 1)
+        round_w2(late(4, 1, 4), bf4, nc.scalar.copy)
+        round_w2(late(5, 1, 5), bf5, nc.vector.tensor_copy)
         for r, pos in enumerate((pos1, pos2, pos3, pos4)):
             back = lists.tile([P, T // LIST_ROWS], U16, name="back%d" % r)
             nc.sync.dma_start(back[:], pos)
             back_lists.append(back)
-            if r % 2 == 1:
-                load_gate(TOKEN_CUTS[0], TOKEN_CUTS[1], r - 1, r + 1)
-        for lo, hi in zip(TOKEN_CUTS[1:], TOKEN_CUTS[2:]):
-            load_gate(lo, hi, 0, TOP)
+        put_results(2, 2, acc23)
+        put_results(6, 2, acc67)
+        for e, w_bf in ((4, bf4), (5, bf5)):
+            quantise_w2((e,), w_bf)
+            put_results(e, 1, second_layer((e,)))
 
         def fetch(lo, hi, r):
-            part = keep.tile([P, hi - lo], F32, name="part%d_%d" % (lo, r))
+            part = ring_tile("part%d_%d" % (lo, r), hi - lo, F32, 1, 4 * (TOP * lo + r * (hi - lo)))
             nc.vector.tensor_tensor(
-                part[:], y[:].indirect(back_lists[r][:, lo // LIST_ROWS : hi // LIST_ROWS]), gates[lo][:, r, :], MULT
+                part[:], y[:].indirect(back_lists[r][:, lo // LIST_ROWS : hi // LIST_ROWS]), gates[r][:, lo:hi], MULT
             )
             return part
 

@@ -28,7 +28,7 @@ WINDOW = 1408
 STREAM_BUFS = 4
 PASS_BYTES = PACK * H * 4
 SLOT_BYTES = PASSES * PASS_BYTES
-W1_LOADS = ((3,), (3,), (3,), (3,), (3,), (3,), (2, 1), (1, 1, 1))
+W1_LOADS = ((3,), (3,), (3,), (2, 1), (1, 1, 1), (1, 1, 1), (1, 1, 1), (1, 1, 1))
 VECTOR_M = 72
 LAST_VECTOR_M = 84
 EARLY_AT = 2

@@ -29,8 +29,8 @@ STREAM_BUFS = 4
 PASS_BYTES = PACK * H * 4
 SLOT_BYTES = PASSES * PASS_BYTES
 W1_LOADS = ((3,), (3,), (3,), (2, 1), (1, 1, 1), (1, 1, 1), (1, 1, 1), (1, 1, 1))
-VECTOR_M = 72
-LAST_VECTOR_M = 84
+VECTOR_M = 62
+LAST_VECTOR_M = 80
 EARLY_AT = 2
 TOKEN_CUTS = (0, 256, 512, 768)
 
@@ -132,7 +132,7 @@ def tile_moe_ecr_mlp_silu_kernel(
             o0 = 0
             for count in W1_LOADS[e]:
                 raw = preloaded if preloaded is not None else load_w1(e, o0, count)
-                steps = [(o0, count)] if count == PASSES else [(o, 1) for o in range(o0, o0 + count)]
+                steps = [(o, 1) for o in range(o0, o0 + count)]
                 for s0, n in steps:
                     last = e == E - 1 and s0 == PASSES - 1
                     if not last:
@@ -146,8 +146,8 @@ def tile_moe_ecr_mlp_silu_kernel(
                     split = LAST_VECTOR_M if last else VECTOR_M
                     nc.vector.tensor_copy(out=dst[:, :, :split], in_=src[:, :, :split])
                     nc.scalar.copy(out=dst[:, :, split:], in_=src[:, :, split:])
-                    codes = coded.tile([P, n * H], U32, name="w1_codes%d" % n, align_bytes=64, bufs=2 if n > 1 else 4)
-                    scales = coded.tile([P, n * H], U8, name="w1_scales%d" % n, align_bytes=64, bufs=2 if n > 1 else 4)
+                    codes = coded.tile([P, n * H], U32, name="w1_codes%d" % n, align_bytes=64, bufs=6)
+                    scales = coded.tile([P, n * H], U8, name="w1_scales%d" % n, align_bytes=64, bufs=6)
                     cuts = (0, H // 2, H) if last else (0, 2 * H, 3 * H) if n > 1 else (0, H)
                     for c0, c1 in zip(cuts, cuts[1:]):
                         nc.vector.quantize_mx(

@@ -29,8 +29,8 @@ STREAM_BUFS = 4
 PASS_BYTES = PACK * H * 4
 SLOT_BYTES = PASSES * PASS_BYTES
 W1_LOADS = ((3,), (3,), (3,), (2, 1), (1, 1, 1), (1, 1, 1), (1, 1, 1), (1, 1, 1))
-VECTOR_M = 62
-LAST_VECTOR_M = 80
+VECTOR_M = 68
+LAST_VECTOR_M = 84
 EARLY_AT = 2
 TOKEN_CUTS = (0, 256, 512, 768)
 
@@ -189,19 +189,26 @@ def tile_moe_ecr_mlp_silu_kernel(
             )
             return raw
 
-        def round_w2(raw, w_bf, copy):
-            copy(
-                out=w_bf.rearrange("p (e c i j) -> p e c j i", c=N // 4, i=4, j=PACK),
-                in_=raw.rearrange("p (e j c i) -> p e c j i", c=N // 4, i=4, j=PACK),
-            )
+        def round_w2(raw, w_bf, copy, pieces=1):
+            dst = w_bf.rearrange("p (e c i j) -> p e c j i", c=N // 4, i=4, j=PACK)
+            src = raw.rearrange("p (e j c i) -> p e c j i", c=N // 4, i=4, j=PACK)
+            step = N // 4 // pieces
+            for c0 in range(0, N // 4, step):
+                copy(out=dst[:, :, c0 : c0 + step], in_=src[:, :, c0 : c0 + step])
 
         w2_codes, w2_scales = {}, {}
 
-        def quantise_w2(experts, w_bf):
+        def quantise_w2(experts, w_bf, pieces=1):
             first, count = experts[0], len(experts)
             codes = keep.tile([P, count * N], U32, name="w2_codes%d" % first, align_bytes=64)
             scales = keep.tile([P, count * N], U8, name="w2_scales%d" % first, align_bytes=64)
-            nc.vector.quantize_mx(out=codes[:].bitcast(FP8X4), scales=scales[:], in_=w_bf)
+            step = count * N // pieces
+            for c0 in range(0, count * N, step):
+                nc.vector.quantize_mx(
+                    out=codes[:, c0 : c0 + step].bitcast(FP8X4),
+                    scales=scales[:, c0 : c0 + step],
+                    in_=w_bf[:, c0 * PACK : (c0 + step) * PACK],
+                )
             for i, e in enumerate(experts):
                 w2_codes[e] = codes[:, i * N : (i + 1) * N]
                 w2_scales[e] = scales[:, i * N : (i + 1) * N]
@@ -238,6 +245,10 @@ def tile_moe_ecr_mlp_silu_kernel(
                 round_w2(load_w2(slice(0, 2), early_raw[:]), early_bf[:], nc.scalar.copy)
                 quantise_w2((0, 1), early_bf[:])
                 put_results(0, 2, second_layer((0, 1)))
+                for r, pos in enumerate((pos1, pos2, pos3, pos4)):
+                    back = lists.tile([P, T // LIST_ROWS], U16, name="back%d" % r)
+                    nc.sync.dma_start(back[:], pos)
+                    back_lists.append(back)
         last_h = keep.tile([P, H], BF16, name="last_h", align_bytes=64)
         activate(E - 1, last_h[:])
 
@@ -258,15 +269,11 @@ def tile_moe_ecr_mlp_silu_kernel(
         acc23 = second_layer((2, 3))
         bf4, bf5 = late_bf(4, 1, 0), late_bf(5, 1, 1)
         round_w2(late(4, 1, 4), bf4, nc.scalar.copy)
-        round_w2(late(5, 1, 5), bf5, nc.vector.tensor_copy)
-        for r, pos in enumerate((pos1, pos2, pos3, pos4)):
-            back = lists.tile([P, T // LIST_ROWS], U16, name="back%d" % r)
-            nc.sync.dma_start(back[:], pos)
-            back_lists.append(back)
+        round_w2(late(5, 1, 5), bf5, nc.vector.tensor_copy, pieces=2)
         put_results(2, 2, acc23)
         put_results(6, 2, acc67)
         for e, w_bf in ((4, bf4), (5, bf5)):
-            quantise_w2((e,), w_bf)
+            quantise_w2((e,), w_bf, pieces=e - 3)
             put_results(e, 1, second_layer((e,)))
 
         def fetch(lo, hi, r):
@@ -290,7 +297,7 @@ def tile_moe_ecr_mlp_silu_kernel(
                         start=(r == 0 and b == 0),
                         stop=(r == TOP - 1 and b == len(blocks) - 1),
                     )
-            by_token = keep.tile([P, hi - lo], F32, name="by_token")
+            by_token = keep.tile([P, hi - lo], F32, name="by_token%d" % lo)
             nc.scalar.copy(out=by_token[:], in_=turned[:])
             upright = psum_t.tile([P, hi - lo], F32, name="upright", tag="turn")
             for cols in blocks:

@@ -24,13 +24,15 @@ P = 128
 PACK = 4
 PASSES = K // (P * PACK)
 LIST_ROWS = 16
+QUADS, QUAD_ROWS, PLANE_ROWS = 4, 32, 4
 WINDOW = 1408
-STREAM_BUFS = 4
+RING_SLOTS = 4
 PASS_BYTES = PACK * H * 4
 SLOT_BYTES = PASSES * PASS_BYTES
 W1_LOADS = ((3,), (3,), (3,), (2, 1), (1, 1, 1), (1, 1, 1), (1, 1, 1), (1, 1, 1))
 VECTOR_M = 68
-LAST_VECTOR_M = 84
+LAST_VECTOR_M = 40
+EARLY_W2 = 2
 EARLY_AT = 2
 TOKEN_CUTS = (0, 256, 512, 768)
 
@@ -53,20 +55,24 @@ def tile_moe_ecr_mlp_silu_kernel(
         nc.vector.memset(token_scales[:].bitcast(I32), 0)
         token_words = keep.tile([P, (PASSES - 1) * T + WINDOW], I32, name="token_words", align_bytes=64)
         nc.vector.memset(token_words[:, PASSES * T :], 0)
-        nc.sync.dma_start(out=token_words[:, : PASSES * T].rearrange("p (o t) -> p o t", o=PASSES), in_=x_words.rearrange("o p t r -> p o (t r)").bitcast(I32))
+        nc.sync.dma_start(
+            out=token_words[:, : PASSES * T].rearrange("p (o t) -> p o t", o=PASSES),
+            in_=x_words.rearrange("o p t r -> p o (t r)").bitcast(I32),
+        )
         slot_list = lists.tile([P, SLOTS // LIST_ROWS], U16, name="slot_list")
         nc.sync.dma_start(slot_list[:], offs)
 
+        scale_rows = [slice(QUAD_ROWS * quad, QUAD_ROWS * quad + PLANE_ROWS * PASSES) for quad in range(QUADS)]
+
         def load_scales():
             staged = keep.tile([P, T // 4], I32, name="staged_scales")
-            for quad in range(4):
-                rows = slice(32 * quad, 32 * quad + 4 * PASSES)
-                nc.sync.dma_start(out=staged[rows, :], in_=x_scales[:, 4 * quad : 4 * quad + 4, :].bitcast(I32))
+            for quad, rows in enumerate(scale_rows):
+                groups = slice(PLANE_ROWS * quad, PLANE_ROWS * (quad + 1))
+                nc.sync.dma_start(out=staged[rows, :], in_=x_scales[:, groups, :].bitcast(I32))
             return staged
 
         def place_scales(staged):
-            for quad in range(4):
-                rows = slice(32 * quad, 32 * quad + 4 * PASSES)
+            for rows in scale_rows:
                 nc.vector.tensor_copy(out=token_scales[rows, :T].bitcast(I32), in_=staged[rows, :])
 
         y = keep.tile([P, SLOTS + PAD], F32, name="y", align_bytes=64)
@@ -80,7 +86,7 @@ def tile_moe_ecr_mlp_silu_kernel(
 
         halves, blocks = 2, T // (2 * P)
         staged_gate = keep.tile([TOP * halves, blocks * P], F32, name="staged_gate")
-        nc.sync.dma_start(out=staged_gate[:], in_=gate[:, 0, :].rearrange("r (h m) -> r h m", h=halves))
+        nc.sync.dma_start(out=staged_gate[:], in_=gate[:, 0, :].rearrange("r (u m) -> r u m", u=halves))
 
         def spread_gate():
             gate_rows = keep.tile([P, blocks * P], F32, name="gate_rows")
@@ -91,18 +97,17 @@ def tile_moe_ecr_mlp_silu_kernel(
                 nc.tensor.transpose(gate_turned[:, b, :], gate_rows[:, b * P : (b + 1) * P], identity[:])
             gate_cols = keep.tile([P, blocks, TOP * halves], F32, name="gate_cols")
             nc.scalar.copy(out=gate_cols[:], in_=gate_turned[:, :, : TOP * halves])
-            for first in range(0, TOP * halves * blocks, 4):
-                spread = psum_t.tile([P, 4 * P], F32, name="spread", tag="turn")
-                for i in range(4):
+            per_bank = 4
+            for first in range(0, TOP * halves * blocks, per_bank):
+                spread = psum_t.tile([P, per_bank * P], F32, name="spread", tag="turn")
+                for i in range(per_bank):
                     row, b = divmod(first + i, blocks)
                     nc.tensor.transpose(
                         spread[:, i * P : (i + 1) * P],
                         gate_cols[:, b, row : row + 1].to_broadcast([P, P]),
                         identity[:],
                     )
-                nc.scalar.copy(out=gate_all[:, first * P : (first + 4) * P], in_=spread[:])
-
-        h_codes, h_scales, sums = {}, {}, {}
+                nc.scalar.copy(out=gate_all[:, first * P : (first + per_bank) * P], in_=spread[:])
 
         slot_words = keep.tile([P, PASSES, SLOTS], U32, name="slot_words", align_bytes=64)
         slot_scales = keep.tile([P, SLOTS], U8, name="slot_scales", align_bytes=64)
@@ -115,61 +120,65 @@ def tile_moe_ecr_mlp_silu_kernel(
         def gather_scales():
             nc.vector.tensor_copy(slot_scales[:], token_scales[:].indirect(slot_list[:]))
 
-        def ring_tile(name, columns, dtype, slot, byte):
-            return ring.tile([P, columns], dtype, name=name, align_bytes=64, offset=slot * SLOT_BYTES + byte)[:]
+        def ring_tile(name, columns, dtype, ring_slot, byte):
+            return ring.tile([P, columns], dtype, name=name, align_bytes=64, offset=ring_slot * SLOT_BYTES + byte)[:]
 
-        def load_w1(e, o0, count):
-            raw = ring_tile("raw%d_%d" % (e, o0), count * PACK * H, F32, e % STREAM_BUFS, o0 * PASS_BYTES)
-            rows = w1[e, o0 * P * PACK : (o0 + count) * P * PACK, :]
+        def load_w1(e, first, count):
+            raw = ring_tile("raw%d_%d" % (e, first), count * PACK * H, F32, e % RING_SLOTS, first * PASS_BYTES)
+            rows = w1[e, first * P * PACK : (first + count) * P * PACK, :]
             nc.sync.dma_start(
                 out=raw.rearrange("p (o x) -> p o x", o=count), in_=rows.rearrange("(o p j) c -> p o (j c)", p=P, j=PACK)
             )
             return raw
 
-        def first_layer(e, preloaded=None):
+        sums, h_codes, h_scales, w2_codes, w2_scales = {}, {}, {}, {}, {}
+
+        def round_w1(raw, w_bf, last):
+            dst = w_bf.rearrange("p (t m j) -> p m j t", t=PACK, j=PACK)
+            src = raw.rearrange("p (j m t) -> p m j t", j=PACK, t=PACK)
+            if last:
+                low, high = slice(0, PACK // 2), slice(PACK // 2, PACK)
+                nc.vector.tensor_copy(out=dst[:, :, :, low], in_=src[:, :, :, low])
+                nc.vector.tensor_copy(out=dst[:, :LAST_VECTOR_M, :, high], in_=src[:, :LAST_VECTOR_M, :, high])
+                nc.scalar.copy(out=dst[:, LAST_VECTOR_M:, :, high], in_=src[:, LAST_VECTOR_M:, :, high])
+            else:
+                nc.vector.tensor_copy(out=dst[:, :VECTOR_M], in_=src[:, :VECTOR_M])
+                nc.scalar.copy(out=dst[:, VECTOR_M:], in_=src[:, VECTOR_M:])
+
+        def first_layer(e, loaded=None):
             slots = slice(e * C, (e + 1) * C)
             acc = psum_a.tile([P, PACK, C], F32, name="acc", tag="acc")
-            o0 = 0
+            first = 0
             for count in W1_LOADS[e]:
-                raw = preloaded if preloaded is not None else load_w1(e, o0, count)
-                steps = [(o, 1) for o in range(o0, o0 + count)]
-                for s0, n in steps:
-                    last = e == E - 1 and s0 == PASSES - 1
+                raw = loaded if loaded is not None else load_w1(e, first, count)
+                for o in range(first, first + count):
+                    last = e == E - 1 and o == PASSES - 1
                     if not last:
-                        w_bf = rounded.tile(
-                            [P, n * H * PACK], BF16, name="w1_bf%d" % n, align_bytes=64, bufs=2 if n > 1 else 4
-                        )
-                    dst = w_bf[:].rearrange("p (o t m j) -> p o m j t", o=n, t=PACK, j=PACK)
-                    src = raw[:, (s0 - o0) * PACK * H : (s0 - o0 + n) * PACK * H].rearrange(
-                        "p (o j m t) -> p o m j t", o=n, j=PACK, t=PACK
-                    )
-                    split = LAST_VECTOR_M if last else VECTOR_M
-                    nc.vector.tensor_copy(out=dst[:, :, :split], in_=src[:, :, :split])
-                    nc.scalar.copy(out=dst[:, :, split:], in_=src[:, :, split:])
-                    codes = coded.tile([P, n * H], U32, name="w1_codes%d" % n, align_bytes=64, bufs=6)
-                    scales = coded.tile([P, n * H], U8, name="w1_scales%d" % n, align_bytes=64, bufs=6)
-                    cuts = (0, H // 2, H) if last else (0, 2 * H, 3 * H) if n > 1 else (0, H)
-                    for c0, c1 in zip(cuts, cuts[1:]):
+                        w_bf = rounded.tile([P, H * PACK], BF16, name="w1_bf", align_bytes=64)
+                    round_w1(raw[:, (o - first) * PACK * H : (o - first + 1) * PACK * H], w_bf[:], last)
+                    codes = coded.tile([P, H], U32, name="w1_codes", align_bytes=64)
+                    scales = coded.tile([P, H], U8, name="w1_scales", align_bytes=64)
+                    width = H // 2 if last else H
+                    for c0 in range(0, H, width):
                         nc.vector.quantize_mx(
-                            out=codes[:, c0:c1].bitcast(FP8X4),
-                            scales=scales[:, c0:c1],
-                            in_=w_bf[:, c0 * PACK : c1 * PACK],
+                            out=codes[:, c0 : c0 + width].bitcast(FP8X4),
+                            scales=scales[:, c0 : c0 + width],
+                            in_=w_bf[:, c0 * PACK : (c0 + width) * PACK],
                         )
-                    for o in range(s0, s0 + n):
-                        for t in range(PACK):
-                            cols = slice((o - s0) * H + t * P, (o - s0) * H + (t + 1) * P)
-                            nc.tensor.matmul_mx(
-                                out=acc[:, t, :],
-                                lhsT=codes[:, cols].bitcast(FP8X4),
-                                lhsT_scale=scales[:, cols],
-                                rhs=slot_words[:, o, slots].bitcast(FP8X4),
-                                rhs_scale=slot_scales[4 * o :, slots],
-                                start=(o == 0 and t == 0),
-                                stop=(o == PASSES - 1 and t == PACK - 1),
-                            )
-                if o0 == 0 and e > 0:
-                    activate(e - 1, ring_tile("h%d" % (e - 1), H, BF16, e % STREAM_BUFS, 0))
-                o0 += count
+                    for t in range(PACK):
+                        cols = slice(t * P, (t + 1) * P)
+                        nc.tensor.matmul_mx(
+                            out=acc[:, t, :],
+                            lhsT=codes[:, cols].bitcast(FP8X4),
+                            lhsT_scale=scales[:, cols],
+                            rhs=slot_words[:, o, slots].bitcast(FP8X4),
+                            rhs_scale=slot_scales[PLANE_ROWS * o :, slots],
+                            start=(o == 0 and t == 0),
+                            stop=(o == PASSES - 1 and t == PACK - 1),
+                        )
+                if first == 0 and e > 0:
+                    activate(e - 1, ring_tile("h%d" % (e - 1), H, BF16, e % RING_SLOTS, 0))
+                first += count
             sums[e] = acc
 
         def activate(e, h_bf):
@@ -178,14 +187,12 @@ def tile_moe_ecr_mlp_silu_kernel(
             )
             h_codes[e] = keep.tile([P, C], U32, name="h_codes%d" % e, align_bytes=64)
             h_scales[e] = keep.tile([P, C], U8, name="h_scales%d" % e, align_bytes=64)
-            nc.vector.quantize_mx(
-                out=h_codes[e][:].bitcast(FP8X4), scales=h_scales[e][:], in_=h_bf
-            )
+            nc.vector.quantize_mx(out=h_codes[e][:].bitcast(FP8X4), scales=h_scales[e][:], in_=h_bf)
 
-        def load_w2(experts, raw):
+        def load_w2(first, count, raw):
             nc.sync.dma_start(
                 out=raw.rearrange("p (e x) -> p e x", x=H),
-                in_=w2[experts].rearrange("e (p j) n -> p e (j n)", j=PACK),
+                in_=w2[first : first + count].rearrange("e (p j) n -> p e (j n)", j=PACK),
             )
             return raw
 
@@ -196,10 +203,7 @@ def tile_moe_ecr_mlp_silu_kernel(
             for c0 in range(0, N // 4, step):
                 copy(out=dst[:, :, c0 : c0 + step], in_=src[:, :, c0 : c0 + step])
 
-        w2_codes, w2_scales = {}, {}
-
-        def quantise_w2(experts, w_bf, pieces=1):
-            first, count = experts[0], len(experts)
+        def quantise_w2(first, count, w_bf, pieces=1):
             codes = keep.tile([P, count * N], U32, name="w2_codes%d" % first, align_bytes=64)
             scales = keep.tile([P, count * N], U8, name="w2_scales%d" % first, align_bytes=64)
             step = count * N // pieces
@@ -209,19 +213,19 @@ def tile_moe_ecr_mlp_silu_kernel(
                     scales=scales[:, c0 : c0 + step],
                     in_=w_bf[:, c0 * PACK : (c0 + step) * PACK],
                 )
-            for i, e in enumerate(experts):
-                w2_codes[e] = codes[:, i * N : (i + 1) * N]
-                w2_scales[e] = scales[:, i * N : (i + 1) * N]
+            for i in range(count):
+                w2_codes[first + i] = codes[:, i * N : (i + 1) * N]
+                w2_scales[first + i] = scales[:, i * N : (i + 1) * N]
 
-        def second_layer(experts):
-            acc = psum_y.tile([P, len(experts) * C], F32, name="acc_y")
-            for i, e in enumerate(experts):
+        def second_layer(first, count):
+            acc = psum_y.tile([P, count * C], F32, name="acc_y")
+            for i in range(count):
                 nc.tensor.matmul_mx(
                     out=acc[:, i * C : (i + 1) * C],
-                    lhsT=w2_codes[e].bitcast(FP8X4),
-                    lhsT_scale=w2_scales[e],
-                    rhs=h_codes[e][:].bitcast(FP8X4),
-                    rhs_scale=h_scales[e][:],
+                    lhsT=w2_codes[first + i].bitcast(FP8X4),
+                    lhsT_scale=w2_scales[first + i],
+                    rhs=h_codes[first + i][:].bitcast(FP8X4),
+                    rhs_scale=h_scales[first + i][:],
                     start=True,
                     stop=True,
                 )
@@ -240,67 +244,67 @@ def tile_moe_ecr_mlp_silu_kernel(
         for e in range(E):
             first_layer(e, first_raw if e == 0 else None)
             if e == EARLY_AT:
-                early_raw = keep.tile([P, 2 * H], F32, name="early_raw")
-                early_bf = keep.tile([P, 2 * H], BF16, name="w2_bf", align_bytes=64)
-                round_w2(load_w2(slice(0, 2), early_raw[:]), early_bf[:], nc.scalar.copy)
-                quantise_w2((0, 1), early_bf[:])
-                put_results(0, 2, second_layer((0, 1)))
+                early_raw = keep.tile([P, EARLY_W2 * H], F32, name="early_raw")
+                early_bf = keep.tile([P, EARLY_W2 * H], BF16, name="w2_bf", align_bytes=64)
+                round_w2(load_w2(0, EARLY_W2, early_raw[:]), early_bf[:], nc.scalar.copy)
+                quantise_w2(0, EARLY_W2, early_bf[:])
+                put_results(0, EARLY_W2, second_layer(0, EARLY_W2))
                 for r, pos in enumerate((pos1, pos2, pos3, pos4)):
                     back = lists.tile([P, T // LIST_ROWS], U16, name="back%d" % r)
                     nc.sync.dma_start(back[:], pos)
                     back_lists.append(back)
         last_h = keep.tile([P, H], BF16, name="last_h", align_bytes=64)
-        activate(E - 1, last_h[:])
 
-        def late(first, count, place):
-            return load_w2(slice(first, first + count), ring_tile("w2_raw%d" % first, count * H, F32, 0, place * H * 4))
+        def late_raw(first, count):
+            byte = (first - EARLY_W2) * H * 4
+            return load_w2(first, count, ring_tile("w2_raw%d" % first, count * H, F32, 0, byte))
 
         def late_bf(first, count, place):
             byte = (PASSES - 1) * PASS_BYTES + place * H * 2
-            return ring_tile("w2_bf%d" % first, count * H, BF16, (E - 1) % STREAM_BUFS, byte)
+            return ring_tile("w2_bf%d" % first, count * H, BF16, (E - 1) % RING_SLOTS, byte)
 
-        bf67, bf23 = late_bf(6, 2, 0), late_bf(2, 2, 2)
-        round_w2(late(6, 2, 0), bf67, nc.scalar.copy)
-        round_w2(late(2, 1, 2), bf23[:, :H], nc.vector.tensor_copy)
-        round_w2(late(3, 1, 3), bf23[:, H:], nc.vector.tensor_copy)
-        quantise_w2((6, 7), bf67)
-        acc67 = second_layer((6, 7))
-        quantise_w2((2, 3), bf23)
-        acc23 = second_layer((2, 3))
-        bf4, bf5 = late_bf(4, 1, 0), late_bf(5, 1, 1)
-        round_w2(late(4, 1, 4), bf4, nc.scalar.copy)
-        round_w2(late(5, 1, 5), bf5, nc.vector.tensor_copy, pieces=2)
-        put_results(2, 2, acc23)
-        put_results(6, 2, acc67)
-        for e, w_bf in ((4, bf4), (5, bf5)):
-            quantise_w2((e,), w_bf, pieces=e - 3)
-            put_results(e, 1, second_layer((e,)))
+        bf23, bf45 = late_bf(2, 2, 0), late_bf(4, 2, 2)
+        round_w2(late_raw(2, 2), bf23, nc.scalar.copy)
+        round_w2(late_raw(4, 1), bf45[:, :H], nc.vector.tensor_copy)
+        round_w2(late_raw(5, 1), bf45[:, H:], nc.vector.tensor_copy)
+        quantise_w2(2, 2, bf23)
+        quantise_w2(4, 2, bf45)
+        acc2345 = second_layer(2, 4)
+        activate(E - 1, last_h[:])
+        bf6, bf7 = late_bf(6, 1, 0), late_bf(7, 1, 1)
+        round_w2(late_raw(6, 1), bf6, nc.scalar.copy)
+        round_w2(late_raw(7, 1), bf7, nc.vector.tensor_copy, pieces=2)
+        put_results(2, 4, acc2345)
+        quantise_w2(6, 1, bf6)
+        put_results(6, 1, second_layer(6, 1))
+        quantise_w2(7, 1, bf7, pieces=2)
+        put_results(7, 1, second_layer(7, 1))
 
         def fetch(lo, hi, r):
             part = ring_tile("part%d_%d" % (lo, r), hi - lo, F32, 1, 4 * (TOP * lo + r * (hi - lo)))
             nc.vector.tensor_tensor(
-                part[:], y[:].indirect(back_lists[r][:, lo // LIST_ROWS : hi // LIST_ROWS]), gates[r][:, lo:hi], MULT
+                part, y[:].indirect(back_lists[r][:, lo // LIST_ROWS : hi // LIST_ROWS]), gates[r][:, lo:hi], MULT
             )
             return part
 
         def combine_on_tensor(lo, hi):
-            blocks = [slice(b, b + P) for b in range(0, hi - lo, P)]
+            token_blocks = [slice(b, b + P) for b in range(0, hi - lo, P)]
             turned = psum_a.tile([P, hi - lo], F32, name="turned", tag="acc")
             for r in range(TOP):
                 part = fetch(lo, hi, r)
-                for b, cols in enumerate(blocks):
+                for b, cols in enumerate(token_blocks):
                     nc.tensor.matmul(
                         turned[:, cols],
                         lhsT=part[:, cols],
                         rhs=identity[:],
                         is_transpose=True,
                         start=(r == 0 and b == 0),
-                        stop=(r == TOP - 1 and b == len(blocks) - 1),
+                        stop=(r == TOP - 1 and b == len(token_blocks) - 1),
                     )
             by_token = keep.tile([P, hi - lo], F32, name="by_token%d" % lo)
             nc.scalar.copy(out=by_token[:], in_=turned[:])
             upright = psum_t.tile([P, hi - lo], F32, name="upright", tag="turn")
-            for cols in blocks:
+            for cols in token_blocks:
                 nc.tensor.transpose(upright[:, cols], by_token[:, cols], identity[:])
             total = keep.tile([P, hi - lo], F32, name="total%d" % lo)
             nc.scalar.copy(out=total[:], in_=upright[:])
@@ -313,14 +317,14 @@ def tile_moe_ecr_mlp_silu_kernel(
                 return total
 
             p0, p1, p2 = fetch(lo, hi, 0), fetch(lo, hi, 1), fetch(lo, hi, 2)
-            s01 = add("s01", p0[:], p1[:])
+            s01 = add("s01", p0, p1)
             p3 = fetch(lo, hi, 3)
             width = (hi - lo) // 2
-            halves_c = [slice(0, width), slice(width, 2 * width)]
-            s012 = [add("s012_%d" % i, s01[:, c], p2[:, c]) for i, c in enumerate(halves_c)]
-            for i, c in enumerate(halves_c):
-                total = add("s0123_%d" % i, s012[i][:], p3[:, c])
-                nc.sync.dma_start(out=out[:, lo + c.start : lo + c.stop], in_=total[:])
+            token_halves = [slice(0, width), slice(width, 2 * width)]
+            s012 = [add("s012_%d" % i, s01[:, cols], p2[:, cols]) for i, cols in enumerate(token_halves)]
+            for i, cols in enumerate(token_halves):
+                total = add("s0123_%d" % i, s012[i][:], p3[:, cols])
+                nc.sync.dma_start(out=out[:, lo + cols.start : lo + cols.stop], in_=total[:])
 
         combine_on_tensor(TOKEN_CUTS[0], TOKEN_CUTS[1])
         combine_on_tensor(TOKEN_CUTS[1], TOKEN_CUTS[2])

@@ -26,14 +26,13 @@ PASSES = K // (P * PACK)
 LIST_ROWS = 16
 QUADS, QUAD_ROWS, PLANE_ROWS = 4, 32, 4
 WINDOW = 1408
-RING_SLOTS = 4
+RING_SLOTS = 16
 PASS_BYTES = PACK * H * 4
-SLOT_BYTES = PASSES * PASS_BYTES
-W1_LOADS = ((3,), (3,), (3,), (2, 1), (1, 1, 1), (1, 1, 1), (1, 1, 1), (1, 1, 1))
+W1_LOADS = (4, 6, 3, 3, 2, 1, 2, 1, 1, 1)
 VECTOR_M = 68
 LAST_VECTOR_M = 40
 EARLY_W2 = 2
-EARLY_AT = 2
+EARLY_AT = 3
 TOKEN_CUTS = (0, 256, 512, 768)
 
 
@@ -121,15 +120,21 @@ def tile_moe_ecr_mlp_silu_kernel(
             nc.vector.tensor_copy(slot_scales[:], token_scales[:].indirect(slot_list[:]))
 
         def ring_tile(name, columns, dtype, ring_slot, byte):
-            return ring.tile([P, columns], dtype, name=name, align_bytes=64, offset=ring_slot * SLOT_BYTES + byte)[:]
+            return ring.tile([P, columns], dtype, name=name, align_bytes=64, offset=ring_slot * PASS_BYTES + byte)[:]
 
-        def load_w1(e, first, count):
-            raw = ring_tile("raw%d_%d" % (e, first), count * PACK * H, F32, e % RING_SLOTS, first * PASS_BYTES)
-            rows = w1[e, first * P * PACK : (first + count) * P * PACK, :]
+        w1_rows = w1.rearrange("e k c -> (e k) c")
+        raw_passes = {}
+
+        def load_w1(first, count):
+            raw = ring_tile("raw%d" % first, count * PACK * H, F32, first % RING_SLOTS, 0)
+            rows = w1_rows[first * P * PACK : (first + count) * P * PACK, :]
             nc.sync.dma_start(
                 out=raw.rearrange("p (o x) -> p o x", o=count), in_=rows.rearrange("(o p j) c -> p o (j c)", p=P, j=PACK)
             )
-            return raw
+            for i in range(count):
+                raw_passes[first + i] = raw[:, i * PACK * H : (i + 1) * PACK * H]
+
+        load_starts = {sum(W1_LOADS[:i]): count for i, count in enumerate(W1_LOADS)}
 
         sums, h_codes, h_scales, w2_codes, w2_scales = {}, {}, {}, {}, {}
 
@@ -145,40 +150,42 @@ def tile_moe_ecr_mlp_silu_kernel(
                 nc.vector.tensor_copy(out=dst[:, :VECTOR_M], in_=src[:, :VECTOR_M])
                 nc.scalar.copy(out=dst[:, VECTOR_M:], in_=src[:, VECTOR_M:])
 
-        def first_layer(e, loaded=None):
+        def first_layer(e):
             slots = slice(e * C, (e + 1) * C)
             acc = psum_a.tile([P, PACK, C], F32, name="acc", tag="acc")
-            first = 0
-            for count in W1_LOADS[e]:
-                raw = loaded if loaded is not None else load_w1(e, first, count)
-                for o in range(first, first + count):
-                    last = e == E - 1 and o == PASSES - 1
-                    if not last:
-                        w_bf = rounded.tile([P, H * PACK], BF16, name="w1_bf", align_bytes=64)
-                    round_w1(raw[:, (o - first) * PACK * H : (o - first + 1) * PACK * H], w_bf[:], last)
-                    codes = coded.tile([P, H], U32, name="w1_codes", align_bytes=64)
-                    scales = coded.tile([P, H], U8, name="w1_scales", align_bytes=64)
-                    width = H // 2 if last else H
-                    for c0 in range(0, H, width):
-                        nc.vector.quantize_mx(
-                            out=codes[:, c0 : c0 + width].bitcast(FP8X4),
-                            scales=scales[:, c0 : c0 + width],
-                            in_=w_bf[:, c0 * PACK : (c0 + width) * PACK],
-                        )
-                    for t in range(PACK):
-                        cols = slice(t * P, (t + 1) * P)
-                        nc.tensor.matmul_mx(
-                            out=acc[:, t, :],
-                            lhsT=codes[:, cols].bitcast(FP8X4),
-                            lhsT_scale=scales[:, cols],
-                            rhs=slot_words[:, o, slots].bitcast(FP8X4),
-                            rhs_scale=slot_scales[PLANE_ROWS * o :, slots],
-                            start=(o == 0 and t == 0),
-                            stop=(o == PASSES - 1 and t == PACK - 1),
-                        )
-                if first == 0 and e > 0:
-                    activate(e - 1, ring_tile("h%d" % (e - 1), H, BF16, e % RING_SLOTS, 0))
-                first += count
+            for o in range(PASSES):
+                g = e * PASSES + o
+                if g not in raw_passes:
+                    load_w1(g, load_starts[g])
+                last = g == E * PASSES - 1
+                if not last:
+                    w_bf = rounded.tile([P, H * PACK], BF16, name="w1_bf", align_bytes=64)
+                round_w1(raw_passes[g], w_bf[:], last)
+                codes = coded.tile([P, H], U32, name="w1_codes", align_bytes=64)
+                scales = coded.tile([P, H], U8, name="w1_scales", align_bytes=64)
+                width = H // 2 if last else H
+                for c0 in range(0, H, width):
+                    nc.vector.quantize_mx(
+                        out=codes[:, c0 : c0 + width].bitcast(FP8X4),
+                        scales=scales[:, c0 : c0 + width],
+                        in_=w_bf[:, c0 * PACK : (c0 + width) * PACK],
+                    )
+                for t in range(PACK):
+                    cols = slice(t * P, (t + 1) * P)
+                    nc.tensor.matmul_mx(
+                        out=acc[:, t, :],
+                        lhsT=codes[:, cols].bitcast(FP8X4),
+                        lhsT_scale=scales[:, cols],
+                        rhs=slot_words[:, o, slots].bitcast(FP8X4),
+                        rhs_scale=slot_scales[PLANE_ROWS * o :, slots],
+                        start=(o == 0 and t == 0),
+                        stop=(o == PASSES - 1 and t == PACK - 1),
+                    )
+                if g + 1 in load_starts:
+                    for done in range(e):
+                        if done not in h_codes:
+                            first_pass = (done + 1) * PASSES
+                            activate(done, ring_tile("h%d" % done, H, BF16, first_pass % RING_SLOTS, 0))
             sums[e] = acc
 
         def activate(e, h_bf):
@@ -234,34 +241,28 @@ def tile_moe_ecr_mlp_silu_kernel(
         def put_results(first, count, acc):
             nc.scalar.copy(out=y[:, first * C : (first + count) * C], in_=acc[:])
 
-        first_raw = load_w1(0, 0, PASSES)
+        load_w1(0, load_starts[0])
         staged_scales = load_scales()
         spread_gate()
         gather_words()
         place_scales(staged_scales)
         gather_scales()
-        back_lists = []
         for e in range(E):
-            first_layer(e, first_raw if e == 0 else None)
+            first_layer(e)
             if e == EARLY_AT:
                 early_raw = keep.tile([P, EARLY_W2 * H], F32, name="early_raw")
                 early_bf = keep.tile([P, EARLY_W2 * H], BF16, name="w2_bf", align_bytes=64)
                 round_w2(load_w2(0, EARLY_W2, early_raw[:]), early_bf[:], nc.scalar.copy)
                 quantise_w2(0, EARLY_W2, early_bf[:])
                 put_results(0, EARLY_W2, second_layer(0, EARLY_W2))
-                for r, pos in enumerate((pos1, pos2, pos3, pos4)):
-                    back = lists.tile([P, T // LIST_ROWS], U16, name="back%d" % r)
-                    nc.sync.dma_start(back[:], pos)
-                    back_lists.append(back)
         last_h = keep.tile([P, H], BF16, name="last_h", align_bytes=64)
 
         def late_raw(first, count):
             byte = (first - EARLY_W2) * H * 4
-            return load_w2(first, count, ring_tile("w2_raw%d" % first, count * H, F32, 0, byte))
+            return load_w2(first, count, ring_tile("w2_raw%d" % first, count * H, F32, 8, byte))
 
         def late_bf(first, count, place):
-            byte = (PASSES - 1) * PASS_BYTES + place * H * 2
-            return ring_tile("w2_bf%d" % first, count * H, BF16, (E - 1) % RING_SLOTS, byte)
+            return ring_tile("w2_bf%d" % first, count * H, BF16, (E * PASSES - 1) % RING_SLOTS, place * H * 2)
 
         bf23, bf45 = late_bf(2, 2, 0), late_bf(4, 2, 2)
         round_w2(late_raw(2, 2), bf23, nc.scalar.copy)
@@ -274,6 +275,11 @@ def tile_moe_ecr_mlp_silu_kernel(
         bf6, bf7 = late_bf(6, 1, 0), late_bf(7, 1, 1)
         round_w2(late_raw(6, 1), bf6, nc.scalar.copy)
         round_w2(late_raw(7, 1), bf7, nc.vector.tensor_copy, pieces=2)
+        back_lists = []
+        for r, pos in enumerate((pos1, pos2, pos3, pos4)):
+            back = lists.tile([P, T // LIST_ROWS], U16, name="back%d" % r)
+            nc.sync.dma_start(back[:], pos)
+            back_lists.append(back)
         put_results(2, 4, acc2345)
         quantise_w2(6, 1, bf6)
         put_results(6, 1, second_layer(6, 1))
@@ -281,7 +287,7 @@ def tile_moe_ecr_mlp_silu_kernel(
         put_results(7, 1, second_layer(7, 1))
 
         def fetch(lo, hi, r):
-            part = ring_tile("part%d_%d" % (lo, r), hi - lo, F32, 1, 4 * (TOP * lo + r * (hi - lo)))
+            part = ring_tile("part%d_%d" % (lo, r), hi - lo, F32, 10, 4 * (TOP * lo + r * (hi - lo)))
             nc.vector.tensor_tensor(
                 part, y[:].indirect(back_lists[r][:, lo // LIST_ROWS : hi // LIST_ROWS]), gates[r][:, lo:hi], MULT
             )

@@ -28,7 +28,7 @@ QUADS, QUAD_ROWS, PLANE_ROWS = 4, 32, 4
 WINDOW = 1408
 RING_SLOTS = 16
 PASS_BYTES = PACK * H * 4
-W1_LOADS = (4, 6, 3, 3, 2, 1, 2, 1, 1, 1)
+W1_LOADS = (2, 4, 4, 3, 3, 2, 1, 1, 1, 1, 1, 1)
 VECTOR_M = 68
 LAST_VECTOR_M = 40
 EARLY_W2 = 2
@@ -83,27 +83,27 @@ def tile_moe_ecr_mlp_silu_kernel(
         gate_all = keep.tile([P, TOP * T], F32, name="gate_all")
         gates = [gate_all[:, r * T : (r + 1) * T] for r in range(TOP)]
 
-        halves, blocks = 2, T // (2 * P)
-        staged_gate = keep.tile([TOP * halves, blocks * P], F32, name="staged_gate")
-        nc.sync.dma_start(out=staged_gate[:], in_=gate[:, 0, :].rearrange("r (u m) -> r u m", u=halves))
-
         def spread_gate():
-            gate_rows = keep.tile([P, blocks * P], F32, name="gate_rows")
+            blocks = T // P
+            step = (N // blocks) * T + P
+            start = (TOP - 1) * T
+            pieces = gate.rearrange("r n t -> (r n t)")[start : start + TOP * blocks * step]
+            staged_gate = keep.tile([TOP * blocks, P], F32, name="staged_gate")
+            nc.sync.dma_start(out=staged_gate[:], in_=pieces.rearrange("(j s) -> j s", s=step)[:, :P])
+            gate_rows = keep.tile([P, P], F32, name="gate_rows")
             nc.gpsimd.memset(gate_rows[:], 0.0)
-            nc.gpsimd.tensor_copy(out=gate_rows[: TOP * halves, :], in_=staged_gate[:])
-            gate_turned = psum_t.tile([P, blocks, P], F32, name="gate_turned", tag="turn")
-            for b in range(blocks):
-                nc.tensor.transpose(gate_turned[:, b, :], gate_rows[:, b * P : (b + 1) * P], identity[:])
-            gate_cols = keep.tile([P, blocks, TOP * halves], F32, name="gate_cols")
-            nc.scalar.copy(out=gate_cols[:], in_=gate_turned[:, :, : TOP * halves])
+            nc.gpsimd.tensor_copy(out=gate_rows[: TOP * blocks, :], in_=staged_gate[:])
+            gate_turned = psum_t.tile([P, P], F32, name="gate_turned", tag="turn")
+            nc.tensor.transpose(gate_turned[:], gate_rows[:], identity[:])
+            gate_cols = keep.tile([P, TOP * blocks], F32, name="gate_cols")
+            nc.scalar.copy(out=gate_cols[:], in_=gate_turned[:, : TOP * blocks])
             per_bank = 4
-            for first in range(0, TOP * halves * blocks, per_bank):
+            for first in range(0, TOP * blocks, per_bank):
                 spread = psum_t.tile([P, per_bank * P], F32, name="spread", tag="turn")
                 for i in range(per_bank):
-                    row, b = divmod(first + i, blocks)
                     nc.tensor.transpose(
                         spread[:, i * P : (i + 1) * P],
-                        gate_cols[:, b, row : row + 1].to_broadcast([P, P]),
+                        gate_cols[:, first + i : first + i + 1].to_broadcast([P, P]),
                         identity[:],
                     )
                 nc.scalar.copy(out=gate_all[:, first * P : (first + per_bank) * P], in_=spread[:])
@@ -242,8 +242,8 @@ def tile_moe_ecr_mlp_silu_kernel(
             nc.scalar.copy(out=y[:, first * C : (first + count) * C], in_=acc[:])
 
         load_w1(0, load_starts[0])
-        staged_scales = load_scales()
         spread_gate()
+        staged_scales = load_scales()
         gather_words()
         place_scales(staged_scales)
         gather_scales()
@@ -266,8 +266,7 @@ def tile_moe_ecr_mlp_silu_kernel(
 
         bf23, bf45 = late_bf(2, 2, 0), late_bf(4, 2, 2)
         round_w2(late_raw(2, 2), bf23, nc.scalar.copy)
-        round_w2(late_raw(4, 1), bf45[:, :H], nc.vector.tensor_copy)
-        round_w2(late_raw(5, 1), bf45[:, H:], nc.vector.tensor_copy)
+        round_w2(late_raw(4, 2), bf45, nc.vector.tensor_copy)
         quantise_w2(2, 2, bf23)
         quantise_w2(4, 2, bf45)
         acc2345 = second_layer(2, 4)

@@ -266,7 +266,8 @@ def tile_moe_ecr_mlp_silu_kernel(
 
         bf23, bf45 = late_bf(2, 2, 0), late_bf(4, 2, 2)
         round_w2(late_raw(2, 2), bf23, nc.scalar.copy)
-        round_w2(late_raw(4, 2), bf45, nc.vector.tensor_copy)
+        round_w2(late_raw(4, 1), bf45[:, :H], nc.vector.tensor_copy)
+        round_w2(late_raw(5, 1), bf45[:, H:], nc.vector.tensor_copy)
         quantise_w2(2, 2, bf23)
         quantise_w2(4, 2, bf45)
         acc2345 = second_layer(2, 4)

@@ -275,11 +275,10 @@ def tile_moe_ecr_mlp_silu_kernel(
         bf6, bf7 = late_bf(6, 1, 0), late_bf(7, 1, 1)
         round_w2(late_raw(6, 1), bf6, nc.scalar.copy)
         round_w2(late_raw(7, 1), bf7, nc.vector.tensor_copy, pieces=2)
-        back_lists = []
-        for r, pos in enumerate((pos1, pos2, pos3, pos4)):
-            back = lists.tile([P, T // LIST_ROWS], U16, name="back%d" % r)
-            nc.sync.dma_start(back[:], pos)
-            back_lists.append(back)
+        back_lists = {}
+        for r, pos in reversed(list(enumerate((pos1, pos2, pos3, pos4)))):
+            back_lists[r] = lists.tile([P, T // LIST_ROWS], U16, name="back%d" % r)
+            nc.sync.dma_start(back_lists[r][:], pos)
         put_results(2, 4, acc2345)
         quantise_w2(6, 1, bf6)
         put_results(6, 1, second_layer(6, 1))
@@ -287,25 +286,25 @@ def tile_moe_ecr_mlp_silu_kernel(
         put_results(7, 1, second_layer(7, 1))
 
         def fetch(lo, hi, r):
-            part = ring_tile("part%d_%d" % (lo, r), hi - lo, F32, 10, 4 * (TOP * lo + r * (hi - lo)))
+            part = ring_tile("part%d_%d" % (lo, r), hi - lo, F32, 10, 4 * (r * T + lo))
             nc.vector.tensor_tensor(
                 part, y[:].indirect(back_lists[r][:, lo // LIST_ROWS : hi // LIST_ROWS]), gates[r][:, lo:hi], MULT
             )
             return part
 
-        def combine_on_tensor(lo, hi):
+        def combine_on_tensor(lo, hi, wide):
             token_blocks = [slice(b, b + P) for b in range(0, hi - lo, P)]
             turned = psum_a.tile([P, hi - lo], F32, name="turned", tag="acc")
-            for r in range(TOP):
-                part = fetch(lo, hi, r)
+            for r in reversed(range(TOP)):
+                part = wide[r][:, lo:hi] if r in wide else fetch(lo, hi, r)
                 for b, cols in enumerate(token_blocks):
                     nc.tensor.matmul(
                         turned[:, cols],
                         lhsT=part[:, cols],
                         rhs=identity[:],
                         is_transpose=True,
-                        start=(r == 0 and b == 0),
-                        stop=(r == TOP - 1 and b == len(token_blocks) - 1),
+                        start=(r == TOP - 1 and b == 0),
+                        stop=(r == 0 and b == len(token_blocks) - 1),
                     )
             by_token = keep.tile([P, hi - lo], F32, name="by_token%d" % lo)
             nc.scalar.copy(out=by_token[:], in_=turned[:])
@@ -332,6 +331,7 @@ def tile_moe_ecr_mlp_silu_kernel(
                 total = add("s0123_%d" % i, s012[i][:], p3[:, cols])
                 nc.sync.dma_start(out=out[:, lo + cols.start : lo + cols.stop], in_=total[:])
 
-        combine_on_tensor(TOKEN_CUTS[0], TOKEN_CUTS[1])
-        combine_on_tensor(TOKEN_CUTS[1], TOKEN_CUTS[2])
+        wide = {r: fetch(TOKEN_CUTS[0], TOKEN_CUTS[2], r) for r in reversed(range(1, TOP))}
+        combine_on_tensor(TOKEN_CUTS[0], TOKEN_CUTS[1], wide)
+        combine_on_tensor(TOKEN_CUTS[1], TOKEN_CUTS[2], wide)
         combine_on_vector(TOKEN_CUTS[2], TOKEN_CUTS[3])

@@ -50,6 +50,15 @@ def tile_moe_ecr_mlp_silu_kernel(
         psum_y = ctx.enter_context(tc.psum_pool(name="psum_y", bufs=4))
         psum_t = ctx.enter_context(tc.psum_pool(name="psum_t", bufs=2))
 
+        def ring_tile(name, columns, dtype, ring_slot, byte):
+            return ring.tile([P, columns], dtype, name=name, align_bytes=64, offset=ring_slot * PASS_BYTES + byte)[:]
+
+        scale_rows = [slice(QUAD_ROWS * quad, QUAD_ROWS * quad + PLANE_ROWS * PASSES) for quad in range(QUADS)]
+        staged_scales = keep.tile([P, T // 4], I32, name="staged_scales")
+        for quad, rows in enumerate(scale_rows):
+            groups = slice(PLANE_ROWS * quad, PLANE_ROWS * (quad + 1))
+            nc.gpsimd.dma_start(out=staged_scales[rows, :], in_=x_scales[:, groups, :].bitcast(I32))
+
         token_scales = keep.tile([P, WINDOW], U8, name="token_scales", align_bytes=64)
         nc.vector.memset(token_scales[:].bitcast(I32), 0)
         token_words = keep.tile([P, (PASSES - 1) * T + WINDOW], I32, name="token_words", align_bytes=64)
@@ -60,15 +69,6 @@ def tile_moe_ecr_mlp_silu_kernel(
         )
         slot_list = lists.tile([P, SLOTS // LIST_ROWS], U16, name="slot_list")
         nc.sync.dma_start(slot_list[:], offs)
-
-        scale_rows = [slice(QUAD_ROWS * quad, QUAD_ROWS * quad + PLANE_ROWS * PASSES) for quad in range(QUADS)]
-
-        def load_scales():
-            staged = keep.tile([P, T // 4], I32, name="staged_scales")
-            for quad, rows in enumerate(scale_rows):
-                groups = slice(PLANE_ROWS * quad, PLANE_ROWS * (quad + 1))
-                nc.sync.dma_start(out=staged[rows, :], in_=x_scales[:, groups, :].bitcast(I32))
-            return staged
 
         def place_scales(staged):
             for rows in scale_rows:
@@ -118,9 +118,6 @@ def tile_moe_ecr_mlp_silu_kernel(
 
         def gather_scales():
             nc.vector.tensor_copy(slot_scales[:], token_scales[:].indirect(slot_list[:]))
-
-        def ring_tile(name, columns, dtype, ring_slot, byte):
-            return ring.tile([P, columns], dtype, name=name, align_bytes=64, offset=ring_slot * PASS_BYTES + byte)[:]
 
         w1_rows = w1.rearrange("e k c -> (e k) c")
         raw_passes = {}
@@ -243,7 +240,6 @@ def tile_moe_ecr_mlp_silu_kernel(
 
         load_w1(0, load_starts[0])
         spread_gate()
-        staged_scales = load_scales()
         gather_words()
         place_scales(staged_scales)
         gather_scales()

@@ -45,7 +45,7 @@ def tile_moe_ecr_mlp_silu_kernel(
         keep = ctx.enter_context(tc.tile_pool(name="keep", bufs=1))
         ring = ctx.enter_context(tc.tile_pool(name="ring", bufs=1))
         rounded = ctx.enter_context(tc.tile_pool(name="rounded", bufs=4))
-        coded = ctx.enter_context(tc.tile_pool(name="coded", bufs=6))
+        coded = ctx.enter_context(tc.tile_pool(name="coded", bufs=8))
         psum_a = ctx.enter_context(tc.psum_pool(name="psum_a", bufs=2))
         psum_y = ctx.enter_context(tc.psum_pool(name="psum_y", bufs=4))
         psum_t = ctx.enter_context(tc.psum_pool(name="psum_t", bufs=2))
@@ -53,14 +53,18 @@ def tile_moe_ecr_mlp_silu_kernel(
         def ring_tile(name, columns, dtype, ring_slot, byte):
             return ring.tile([P, columns], dtype, name=name, align_bytes=64, offset=ring_slot * PASS_BYTES + byte)[:]
 
+        identity = keep.tile([P, P], F32, name="identity")
+        make_identity(nc, identity[:])
+
+        gate_rows = keep.tile([P, P], F32, name="gate_rows")
+        nc.gpsimd.memset(gate_rows[:], 0.0)
+
         scale_rows = [slice(QUAD_ROWS * quad, QUAD_ROWS * quad + PLANE_ROWS * PASSES) for quad in range(QUADS)]
         staged_scales = keep.tile([P, T // 4], I32, name="staged_scales")
         for quad, rows in enumerate(scale_rows):
             groups = slice(PLANE_ROWS * quad, PLANE_ROWS * (quad + 1))
             nc.gpsimd.dma_start(out=staged_scales[rows, :], in_=x_scales[:, groups, :].bitcast(I32))
 
-        token_scales = keep.tile([P, WINDOW], U8, name="token_scales", align_bytes=64)
-        nc.vector.memset(token_scales[:].bitcast(I32), 0)
         token_words = keep.tile([P, (PASSES - 1) * T + WINDOW], I32, name="token_words", align_bytes=64)
         nc.vector.memset(token_words[:, PASSES * T :], 0)
         nc.sync.dma_start(
@@ -70,15 +74,9 @@ def tile_moe_ecr_mlp_silu_kernel(
         slot_list = lists.tile([P, SLOTS // LIST_ROWS], U16, name="slot_list")
         nc.sync.dma_start(slot_list[:], offs)
 
-        def place_scales(staged):
-            for rows in scale_rows:
-                nc.vector.tensor_copy(out=token_scales[rows, :T].bitcast(I32), in_=staged[rows, :])
 
         y = keep.tile([P, SLOTS + PAD], F32, name="y", align_bytes=64)
         nc.vector.memset(y[:, SLOTS:], 0.0)
-
-        identity = keep.tile([P, P], F32, name="identity")
-        make_identity(nc, identity[:])
 
         gate_all = keep.tile([P, TOP * T], F32, name="gate_all")
         gates = [gate_all[:, r * T : (r + 1) * T] for r in range(TOP)]
@@ -90,9 +88,7 @@ def tile_moe_ecr_mlp_silu_kernel(
             pieces = gate.rearrange("r n t -> (r n t)")[start : start + TOP * blocks * step]
             staged_gate = keep.tile([TOP * blocks, P], F32, name="staged_gate")
             nc.sync.dma_start(out=staged_gate[:], in_=pieces.rearrange("(j s) -> j s", s=step)[:, :P])
-            gate_rows = keep.tile([P, P], F32, name="gate_rows")
-            nc.gpsimd.memset(gate_rows[:], 0.0)
-            nc.gpsimd.tensor_copy(out=gate_rows[: TOP * blocks, :], in_=staged_gate[:])
+            nc.scalar.copy(out=gate_rows[: TOP * blocks, :], in_=staged_gate[:])
             gate_turned = psum_t.tile([P, P], F32, name="gate_turned", tag="turn")
             nc.tensor.transpose(gate_turned[:], gate_rows[:], identity[:])
             gate_cols = keep.tile([P, TOP * blocks], F32, name="gate_cols")
@@ -117,7 +113,11 @@ def tile_moe_ecr_mlp_silu_kernel(
                 nc.vector.tensor_copy(slot_words[:, o, :], window.indirect(slot_list[:]))
 
         def gather_scales():
-            nc.vector.tensor_copy(slot_scales[:], token_scales[:].indirect(slot_list[:]))
+            token_scales = ring_tile("token_scales", WINDOW, U8, W1_LOADS[0], 0)
+            nc.vector.memset(token_scales.bitcast(I32), 0)
+            for rows in scale_rows:
+                nc.vector.tensor_copy(out=token_scales[rows, :T].bitcast(I32), in_=staged_scales[rows, :])
+            nc.vector.tensor_copy(slot_scales[:], token_scales.indirect(slot_list[:]))
 
         w1_rows = w1.rearrange("e k c -> (e k) c")
         raw_passes = {}
@@ -147,6 +147,22 @@ def tile_moe_ecr_mlp_silu_kernel(
                 nc.vector.tensor_copy(out=dst[:, :VECTOR_M], in_=src[:, :VECTOR_M])
                 nc.scalar.copy(out=dst[:, VECTOR_M:], in_=src[:, VECTOR_M:])
 
+        def multiply(acc, slots, o, codes, scales):
+            for t in range(PACK):
+                cols = slice(t * P, (t + 1) * P)
+                nc.tensor.matmul_mx(
+                    out=acc[:, t, :],
+                    lhsT=codes[:, cols].bitcast(FP8X4),
+                    lhsT_scale=scales[:, cols],
+                    rhs=slot_words[:, o, slots].bitcast(FP8X4),
+                    rhs_scale=slot_scales[PLANE_ROWS * o :, slots],
+                    start=(o == 0 and t == 0),
+                    stop=(o == PASSES - 1 and t == PACK - 1),
+                )
+
+        waiting = []
+        first_multiplied = W1_LOADS[0] + W1_LOADS[1] - 1
+
         def first_layer(e):
             slots = slice(e * C, (e + 1) * C)
             acc = psum_a.tile([P, PACK, C], F32, name="acc", tag="acc")
@@ -167,18 +183,14 @@ def tile_moe_ecr_mlp_silu_kernel(
                         scales=scales[:, c0 : c0 + width],
                         in_=w_bf[:, c0 * PACK : (c0 + width) * PACK],
                     )
-                for t in range(PACK):
-                    cols = slice(t * P, (t + 1) * P)
-                    nc.tensor.matmul_mx(
-                        out=acc[:, t, :],
-                        lhsT=codes[:, cols].bitcast(FP8X4),
-                        lhsT_scale=scales[:, cols],
-                        rhs=slot_words[:, o, slots].bitcast(FP8X4),
-                        rhs_scale=slot_scales[PLANE_ROWS * o :, slots],
-                        start=(o == 0 and t == 0),
-                        stop=(o == PASSES - 1 and t == PACK - 1),
-                    )
-                if g + 1 in load_starts:
+                waiting.append((acc, slots, o, codes, scales))
+                if g == first_multiplied:
+                    gather_scales()
+                if g >= first_multiplied:
+                    for job in waiting:
+                        multiply(*job)
+                    waiting.clear()
+                if g + 1 in load_starts and g > first_multiplied:
                     for done in range(e):
                         if done not in h_codes:
                             first_pass = (done + 1) * PASSES
@@ -241,8 +253,6 @@ def tile_moe_ecr_mlp_silu_kernel(
         load_w1(0, load_starts[0])
         spread_gate()
         gather_words()
-        place_scales(staged_scales)
-        gather_scales()
         for e in range(E):
             first_layer(e)
             if e == EARLY_AT:

@@ -45,7 +45,7 @@ def tile_moe_ecr_mlp_silu_kernel(
         keep = ctx.enter_context(tc.tile_pool(name="keep", bufs=1))
         ring = ctx.enter_context(tc.tile_pool(name="ring", bufs=1))
         rounded = ctx.enter_context(tc.tile_pool(name="rounded", bufs=4))
-        coded = ctx.enter_context(tc.tile_pool(name="coded", bufs=8))
+        coded = ctx.enter_context(tc.tile_pool(name="coded", bufs=6))
         psum_a = ctx.enter_context(tc.psum_pool(name="psum_a", bufs=2))
         psum_y = ctx.enter_context(tc.psum_pool(name="psum_y", bufs=4))
         psum_t = ctx.enter_context(tc.psum_pool(name="psum_t", bufs=2))
@@ -113,7 +113,7 @@ def tile_moe_ecr_mlp_silu_kernel(
                 nc.vector.tensor_copy(slot_words[:, o, :], window.indirect(slot_list[:]))
 
         def gather_scales():
-            token_scales = ring_tile("token_scales", WINDOW, U8, W1_LOADS[0], 0)
+            token_scales = ring_tile("token_scales", WINDOW, U8, 0, 0)
             nc.vector.memset(token_scales.bitcast(I32), 0)
             for rows in scale_rows:
                 nc.vector.tensor_copy(out=token_scales[rows, :T].bitcast(I32), in_=staged_scales[rows, :])
@@ -161,7 +161,7 @@ def tile_moe_ecr_mlp_silu_kernel(
                 )
 
         waiting = []
-        first_multiplied = W1_LOADS[0] + W1_LOADS[1] - 1
+        first_multiplied = W1_LOADS[0] - 1
 
         def first_layer(e):
             slots = slice(e * C, (e + 1) * C)
@@ -190,7 +190,7 @@ def tile_moe_ecr_mlp_silu_kernel(
                     for job in waiting:
                         multiply(*job)
                     waiting.clear()
-                if g + 1 in load_starts and g > first_multiplied:
+                if g + 1 in load_starts:
                     for done in range(e):
                         if done not in h_codes:
                             first_pass = (done + 1) * PASSES

@@ -28,7 +28,7 @@ QUADS, QUAD_ROWS, PLANE_ROWS = 4, 32, 4
 WINDOW = 1408
 RING_SLOTS = 16
 PASS_BYTES = PACK * H * 4
-W1_LOADS = (2, 4, 4, 3, 3, 2, 1, 1, 1, 1, 1, 1)
+W1_LOADS = (2, 2, 2, 2, 2, 2, 2, 2, 1, 1, 1, 1, 1, 1, 1, 1)
 VECTOR_M = 68
 LAST_VECTOR_M = 40
 EARLY_W2 = 2

@@ -28,7 +28,8 @@ QUADS, QUAD_ROWS, PLANE_ROWS = 4, 32, 4
 WINDOW = 1408
 RING_SLOTS = 16
 PASS_BYTES = PACK * H * 4
-W1_LOADS = (2, 2, 2, 2, 2, 2, 2, 2, 1, 1, 1, 1, 1, 1, 1, 1)
+LATE_W2_SLOT, PARTS_SLOT = 8, 10
+W1_LOADS = (2,) * 8 + (1,) * 8
 VECTOR_M = 68
 LAST_VECTOR_M = 40
 EARLY_W2 = 2
@@ -74,7 +75,6 @@ def tile_moe_ecr_mlp_silu_kernel(
         slot_list = lists.tile([P, SLOTS // LIST_ROWS], U16, name="slot_list")
         nc.sync.dma_start(slot_list[:], offs)
 
-
         y = keep.tile([P, SLOTS + PAD], F32, name="y", align_bytes=64)
         nc.vector.memset(y[:, SLOTS:], 0.0)
 
@@ -113,7 +113,7 @@ def tile_moe_ecr_mlp_silu_kernel(
                 nc.vector.tensor_copy(slot_words[:, o, :], window.indirect(slot_list[:]))
 
         def gather_scales():
-            token_scales = ring_tile("token_scales", WINDOW, U8, 0, 0)
+            token_scales = ring_tile("token_scales", WINDOW, U8, W1_LOADS[0], 0)
             nc.vector.memset(token_scales.bitcast(I32), 0)
             for rows in scale_rows:
                 nc.vector.tensor_copy(out=token_scales[rows, :T].bitcast(I32), in_=staged_scales[rows, :])
@@ -161,7 +161,7 @@ def tile_moe_ecr_mlp_silu_kernel(
                 )
 
         waiting = []
-        first_multiplied = W1_LOADS[0] - 1
+        first_multiplied = sum(W1_LOADS[:2]) - 1
 
         def first_layer(e):
             slots = slice(e * C, (e + 1) * C)
@@ -190,7 +190,7 @@ def tile_moe_ecr_mlp_silu_kernel(
                     for job in waiting:
                         multiply(*job)
                     waiting.clear()
-                if g + 1 in load_starts:
+                if g + 1 in load_starts and g >= first_multiplied:
                     for done in range(e):
                         if done not in h_codes:
                             first_pass = (done + 1) * PASSES
@@ -265,7 +265,7 @@ def tile_moe_ecr_mlp_silu_kernel(
 
         def late_raw(first, count):
             byte = (first - EARLY_W2) * H * 4
-            return load_w2(first, count, ring_tile("w2_raw%d" % first, count * H, F32, 8, byte))
+            return load_w2(first, count, ring_tile("w2_raw%d" % first, count * H, F32, LATE_W2_SLOT, byte))
 
         def late_bf(first, count, place):
             return ring_tile("w2_bf%d" % first, count * H, BF16, (E * PASSES - 1) % RING_SLOTS, place * H * 2)
@@ -292,7 +292,7 @@ def tile_moe_ecr_mlp_silu_kernel(
         put_results(7, 1, second_layer(7, 1))
 
         def fetch(lo, hi, r):
-            part = ring_tile("part%d_%d" % (lo, r), hi - lo, F32, 10, 4 * (r * T + lo))
+            part = ring_tile("part%d_%d" % (lo, r), hi - lo, F32, PARTS_SLOT, 4 * (r * T + lo))
             nc.vector.tensor_tensor(
                 part, y[:].indirect(back_lists[r][:, lo // LIST_ROWS : hi // LIST_ROWS]), gates[r][:, lo:hi], MULT
             )

@@ -19,6 +19,7 @@ FP8X4 = mybir.dt.float8_e4m3fn_x4
 MULT = mybir.AluOpType.mult
 ADD = mybir.AluOpType.add
 SILU = mybir.ActivationFunctionType.Silu
+COPY = mybir.ActivationFunctionType.Copy
 
 P = 128
 PACK = 4
@@ -28,13 +29,15 @@ QUADS, QUAD_ROWS, PLANE_ROWS = 4, 32, 4
 WINDOW = 1408
 RING_SLOTS = 16
 PASS_BYTES = PACK * H * 4
-LATE_W2_SLOT, PARTS_SLOT = 8, 10
+LATE_W2_SLOT, PARTS_SLOT, PICKED_SLOT, WEIGHED_SLOT = 8, 10, 12, 14
 W1_LOADS = (2,) * 8 + (1,) * 8
 VECTOR_M = 68
 LAST_VECTOR_M = 40
 EARLY_W2 = 2
 EARLY_AT = 3
-TOKEN_CUTS = (0, 256, 512, 768)
+LAST_CUT = 256
+FIRST_PICK = 256
+TOKEN_CUTS = (0, 384, 768)
 
 
 def tile_moe_ecr_mlp_silu_kernel(
@@ -49,7 +52,7 @@ def tile_moe_ecr_mlp_silu_kernel(
         coded = ctx.enter_context(tc.tile_pool(name="coded", bufs=6))
         psum_a = ctx.enter_context(tc.psum_pool(name="psum_a", bufs=2))
         psum_y = ctx.enter_context(tc.psum_pool(name="psum_y", bufs=4))
-        psum_t = ctx.enter_context(tc.psum_pool(name="psum_t", bufs=2))
+        psum_g = ctx.enter_context(tc.psum_pool(name="psum_g", bufs=1))
 
         def ring_tile(name, columns, dtype, ring_slot, byte):
             return ring.tile([P, columns], dtype, name=name, align_bytes=64, offset=ring_slot * PASS_BYTES + byte)[:]
@@ -81,6 +84,8 @@ def tile_moe_ecr_mlp_silu_kernel(
         gate_all = keep.tile([P, TOP * T], F32, name="gate_all")
         gates = [gate_all[:, r * T : (r + 1) * T] for r in range(TOP)]
 
+        held_gates = {}
+
         def spread_gate():
             blocks = T // P
             step = (N // blocks) * T + P
@@ -89,20 +94,29 @@ def tile_moe_ecr_mlp_silu_kernel(
             staged_gate = keep.tile([TOP * blocks, P], F32, name="staged_gate")
             nc.sync.dma_start(out=staged_gate[:], in_=pieces.rearrange("(j s) -> j s", s=step)[:, :P])
             nc.scalar.copy(out=gate_rows[: TOP * blocks, :], in_=staged_gate[:])
-            gate_turned = psum_t.tile([P, P], F32, name="gate_turned", tag="turn")
+            gate_turned = psum_y.tile([P, P], F32, name="gate_turned", tag="acc_y")
             nc.tensor.transpose(gate_turned[:], gate_rows[:], identity[:])
             gate_cols = keep.tile([P, TOP * blocks], F32, name="gate_cols")
             nc.scalar.copy(out=gate_cols[:], in_=gate_turned[:, : TOP * blocks])
-            per_bank = 4
-            for first in range(0, TOP * blocks, per_bank):
-                spread = psum_t.tile([P, per_bank * P], F32, name="spread", tag="turn")
-                for i in range(per_bank):
+            def spread_blocks(bank, first, count):
+                for i in range(count):
                     nc.tensor.transpose(
-                        spread[:, i * P : (i + 1) * P],
+                        bank[:, i * P : (i + 1) * P],
                         gate_cols[:, first + i : first + i + 1].to_broadcast([P, P]),
                         identity[:],
                     )
-                nc.scalar.copy(out=gate_all[:, first * P : (first + per_bank) * P], in_=spread[:])
+
+            turned_blocks = TOKEN_CUTS[1] // P
+            runs = [(r * blocks, turned_blocks) for r in range(2)] + [(first, 4) for first in range(2 * blocks, TOP * blocks, 4)]
+            for first, count in runs:
+                spread = psum_y.tile([P, count * P], F32, name="spread", tag="acc_y")
+                spread_blocks(spread, first, count)
+                nc.scalar.copy(out=gate_all[:, first * P : (first + count) * P], in_=spread[:])
+            cuts = (turned_blocks, turned_blocks + LAST_CUT // P, blocks)
+            for i, (b0, b1) in enumerate(zip(cuts, cuts[1:])):
+                held_gates[i] = psum_g.tile([P, 2, (b1 - b0) * P], F32, name="held_gate%d" % i)
+                for r in range(2):
+                    spread_blocks(held_gates[i][:, r, :], r * blocks + b0, b1 - b0)
 
         slot_words = keep.tile([P, PASSES, SLOTS], U32, name="slot_words", align_bytes=64)
         slot_scales = keep.tile([P, SLOTS], U8, name="slot_scales", align_bytes=64)
@@ -250,6 +264,12 @@ def tile_moe_ecr_mlp_silu_kernel(
         def put_results(first, count, acc):
             nc.scalar.copy(out=y[:, first * C : (first + count) * C], in_=acc[:])
 
+        back_lists = {}
+
+        def load_back_list(r):
+            back_lists[r] = lists.tile([P, T // LIST_ROWS], U16, name="back%d" % r)
+            nc.sync.dma_start(back_lists[r][:], (pos1, pos2, pos3, pos4)[r])
+
         load_w1(0, load_starts[0])
         spread_gate()
         gather_words()
@@ -276,68 +296,97 @@ def tile_moe_ecr_mlp_silu_kernel(
         round_w2(late_raw(5, 1), bf45[:, H:], nc.vector.tensor_copy)
         quantise_w2(2, 2, bf23)
         quantise_w2(4, 2, bf45)
-        acc2345 = second_layer(2, 4)
+        acc23, acc45 = second_layer(2, 2), second_layer(4, 2)
         activate(E - 1, last_h[:])
         bf6, bf7 = late_bf(6, 1, 0), late_bf(7, 1, 1)
         round_w2(late_raw(6, 1), bf6, nc.scalar.copy)
         round_w2(late_raw(7, 1), bf7, nc.vector.tensor_copy, pieces=2)
-        back_lists = {}
-        for r, pos in reversed(list(enumerate((pos1, pos2, pos3, pos4)))):
-            back_lists[r] = lists.tile([P, T // LIST_ROWS], U16, name="back%d" % r)
-            nc.sync.dma_start(back_lists[r][:], pos)
-        put_results(2, 4, acc2345)
+        for r in (3, 2, 0, 1):
+            load_back_list(r)
+        put_results(2, 2, acc23)
+        put_results(4, 2, acc45)
         quantise_w2(6, 1, bf6)
         put_results(6, 1, second_layer(6, 1))
         quantise_w2(7, 1, bf7, pieces=2)
         put_results(7, 1, second_layer(7, 1))
 
-        def fetch(lo, hi, r):
-            part = ring_tile("part%d_%d" % (lo, r), hi - lo, F32, PARTS_SLOT, 4 * (r * T + lo))
-            nc.vector.tensor_tensor(
-                part, y[:].indirect(back_lists[r][:, lo // LIST_ROWS : hi // LIST_ROWS]), gates[r][:, lo:hi], MULT
-            )
+        def part_tile(name, ring_slot, lo, hi, r, lists=1):
+            return ring_tile("%s%d_%d" % (name, lo, r), lists * (hi - lo), F32, ring_slot, 4 * (TOP * lo + r * (hi - lo)))
+
+        def offsets(lo, hi, r):
+            return back_lists[r][:, lo // LIST_ROWS : hi // LIST_ROWS]
+
+        def fetch(lo, hi, r, part):
+            nc.vector.tensor_tensor(part, y[:].indirect(offsets(lo, hi, r)), gates[r][:, lo:hi], MULT)
             return part
 
-        def combine_on_tensor(lo, hi, wide):
-            token_blocks = [slice(b, b + P) for b in range(0, hi - lo, P)]
-            turned = psum_a.tile([P, hi - lo], F32, name="turned", tag="acc")
-            for r in reversed(range(TOP)):
-                part = wide[r][:, lo:hi] if r in wide else fetch(lo, hi, r)
-                for b, cols in enumerate(token_blocks):
-                    nc.tensor.matmul(
-                        turned[:, cols],
-                        lhsT=part[:, cols],
-                        rhs=identity[:],
-                        is_transpose=True,
-                        start=(r == TOP - 1 and b == 0),
-                        stop=(r == 0 and b == len(token_blocks) - 1),
-                    )
-            by_token = keep.tile([P, hi - lo], F32, name="by_token%d" % lo)
+        def pick(lo, hi, r, picked):
+            nc.scalar.activation(picked, y[:].indirect(offsets(lo, hi, r)), COPY)
+            return picked
+
+        def turn_and_sum(cols, parts):
+            turned = psum_y.tile([P, P], F32, name="acc_y")
+            for i, part in enumerate(parts):
+                nc.tensor.matmul(
+                    turned[:], lhsT=part[:, cols], rhs=identity[:], is_transpose=True, start=(i == 0), stop=(i == TOP - 1)
+                )
+            by_token = keep.tile([P, P], F32, name="by_token%d" % cols.start)
             nc.scalar.copy(out=by_token[:], in_=turned[:])
-            upright = psum_t.tile([P, hi - lo], F32, name="upright", tag="turn")
-            for cols in token_blocks:
-                nc.tensor.transpose(upright[:, cols], by_token[:, cols], identity[:])
-            total = keep.tile([P, hi - lo], F32, name="total%d" % lo)
-            nc.scalar.copy(out=total[:], in_=upright[:])
-            nc.scalar.dma_start(out=out[:, lo:hi], in_=total[:])
+            return by_token
 
-        def combine_on_vector(lo, hi):
-            def add(name, a, b):
-                total = keep.tile([P, a.shape[1]], F32, name=name)
-                nc.vector.tensor_tensor(total[:], a, b, ADD)
-                return total
+        def turn_back(by_token, total, pool, tag):
+            upright = pool.tile([P, P], F32, name="upright", tag=tag)
+            nc.tensor.transpose(upright[:], by_token[:], identity[:])
+            nc.scalar.copy(out=total, in_=upright[:])
 
-            p0, p1, p2 = fetch(lo, hi, 0), fetch(lo, hi, 1), fetch(lo, hi, 2)
-            s01 = add("s01", p0, p1)
-            p3 = fetch(lo, hi, 3)
-            width = (hi - lo) // 2
-            token_halves = [slice(0, width), slice(width, 2 * width)]
-            s012 = [add("s012_%d" % i, s01[:, cols], p2[:, cols]) for i, cols in enumerate(token_halves)]
-            for i, cols in enumerate(token_halves):
-                total = add("s0123_%d" % i, s012[i][:], p3[:, cols])
-                nc.sync.dma_start(out=out[:, lo + cols.start : lo + cols.stop], in_=total[:])
+        def add(name, a, b):
+            total = keep.tile([P, a.shape[1]], F32, name=name)
+            nc.vector.tensor_tensor(total[:], a, b, ADD)
+            return total[:]
 
-        wide = {r: fetch(TOKEN_CUTS[0], TOKEN_CUTS[2], r) for r in reversed(range(1, TOP))}
-        combine_on_tensor(TOKEN_CUTS[0], TOKEN_CUTS[1], wide)
-        combine_on_tensor(TOKEN_CUTS[1], TOKEN_CUTS[2], wide)
-        combine_on_vector(TOKEN_CUTS[2], TOKEN_CUTS[3])
+        def weigh(picked, weights, part):
+            nc.vector.tensor_tensor(part, picked, weights, MULT)
+            return part
+
+        first, lo, hi = TOKEN_CUTS
+        width = hi - lo
+        picked = part_tile("picked", PICKED_SLOT, first, lo, 0, lists=3)
+        pieces = [slice(first, FIRST_PICK), slice(FIRST_PICK, lo)]
+        for cols in pieces:
+            pick(cols.start, cols.stop, 0, picked[:, cols])
+        picked_last = part_tile("picked", PICKED_SLOT, lo, hi, 0, lists=2)
+        for r in range(2):
+            pick(lo, hi, r, picked_last[:, r * width : (r + 1) * width])
+        wide = [fetch(first, lo, r, part_tile("part", PARTS_SLOT, first, lo, r)) for r in (3, 2)]
+        wide.append(part_tile("weighed", WEIGHED_SLOT, first, lo, 0))
+        for cols in pieces:
+            weigh(picked[:, cols], gates[0][:, cols], wide[2][:, cols])
+        wide.append(fetch(first, lo, 1, part_tile("part", PARTS_SLOT, first, lo, 1)))
+        blocks = [slice(b, b + P) for b in range(first, lo, P)]
+        sums_by_token = [turn_and_sum(cols, wide) for cols in blocks]
+        turned_total = keep.tile([P, lo - first], F32, name="turned_total")
+        for cols, by_token, bank in zip(blocks, sums_by_token, ((psum_a, "acc"), (psum_a, "acc"), (psum_y, "acc_y"))):
+            turn_back(by_token, turned_total[:, cols], *bank)
+        nc.scalar.dma_start(out=out[:, first:lo], in_=turned_total[:])
+
+        p3 = fetch(lo, hi, 3, part_tile("last", PICKED_SLOT, first, lo, 0))
+        p2 = fetch(lo, hi, 2, part_tile("last", PICKED_SLOT, first, lo, 1))
+        halves = [slice(0, LAST_CUT), slice(LAST_CUT, width)]
+        s23 = [
+            keep.tile([P, LAST_CUT], F32, name="s23")[:],
+            part_tile("s23", PICKED_SLOT, lo, hi, 1)[:, : width - LAST_CUT],
+        ]
+        nc.gpsimd.tensor_tensor(s23[0], p2[:, halves[0]], p3[:, halves[0]], ADD)
+        products = [
+            ring_tile("products0", 2 * LAST_CUT, F32, PICKED_SLOT, 4 * 2 * (lo - first)),
+            ring_tile("products1", 2 * (width - LAST_CUT), F32, WEIGHED_SLOT + 1, 0),
+        ]
+        products = [both.rearrange("p (r t) -> p r t", r=2) for both in products]
+        for i, cols in enumerate(halves):
+            weigh(picked_last.rearrange("p (r t) -> p r t", r=2)[:, :, cols], held_gates[i][:], products[i])
+        s01 = [add("s01_0", products[0][:, 0, :], products[0][:, 1, :])]
+        nc.vector.tensor_tensor(s23[1], p2[:, halves[1]], p3[:, halves[1]], ADD)
+        s01.append(add("s01_1", products[1][:, 0, :], products[1][:, 1, :]))
+        for i, cols in enumerate(halves):
+            total = add("s0123_%d" % i, s01[i], s23[i])
+            nc.sync.dma_start(out=out[:, lo + cols.start : lo + cols.stop], in_=total)

from contextlib import ExitStack

import concourse.mybir as mybir
from concourse.masks import make_identity

K, T, E, C, H, N = 1536, 768, 8, 128, 512, 128
TOP = 4
PAD = 64
SLOTS = E * C
FLOPS = 2 * SLOTS * (K * H + H * N)

F32 = mybir.dt.float32
BF16 = mybir.dt.bfloat16
I32 = mybir.dt.int32
U32 = mybir.dt.uint32
U16 = mybir.dt.uint16
U8 = mybir.dt.uint8
FP8X4 = mybir.dt.float8_e4m3fn_x4
MULT = mybir.AluOpType.mult
ADD = mybir.AluOpType.add
SILU = mybir.ActivationFunctionType.Silu
COPY = mybir.ActivationFunctionType.Copy

P = 128
PACK = 4
PASSES = K // (P * PACK)
LIST_ROWS = 16
QUADS, QUAD_ROWS, PLANE_ROWS = 4, 32, 4
WINDOW = 1408
RING_SLOTS = 16
PASS_BYTES = PACK * H * 4
LATE_W2_SLOT, PARTS_SLOT, PICKED_SLOT, WEIGHED_SLOT = 8, 10, 12, 14
W1_LOADS = (2,) * 8 + (1,) * 8
VECTOR_M = 68
LAST_VECTOR_M = 40
EARLY_W2 = 2
EARLY_AT = 3
LAST_CUT = 256
FIRST_PICK = 256
TOKEN_CUTS = (0, 384, 768)


def tile_moe_ecr_mlp_silu_kernel(
    tc, x_words, x_scales, w1, w2, gate, offs, pos1, pos2, pos3, pos4, out
):
    nc = tc.nc
    with ExitStack() as ctx:
        lists = ctx.enter_context(tc.tile_pool(name="lists", bufs=1))
        keep = ctx.enter_context(tc.tile_pool(name="keep", bufs=1))
        ring = ctx.enter_context(tc.tile_pool(name="ring", bufs=1))
        rounded = ctx.enter_context(tc.tile_pool(name="rounded", bufs=4))
        coded = ctx.enter_context(tc.tile_pool(name="coded", bufs=6))
        psum_a = ctx.enter_context(tc.psum_pool(name="psum_a", bufs=2))
        psum_y = ctx.enter_context(tc.psum_pool(name="psum_y", bufs=4))
        psum_g = ctx.enter_context(tc.psum_pool(name="psum_g", bufs=1))

        def ring_tile(name, columns, dtype, ring_slot, byte):
            return ring.tile([P, columns], dtype, name=name, align_bytes=64, offset=ring_slot * PASS_BYTES + byte)[:]

        identity = keep.tile([P, P], F32, name="identity")
        make_identity(nc, identity[:])

        gate_rows = keep.tile([P, P], F32, name="gate_rows")
        nc.gpsimd.memset(gate_rows[:], 0.0)

        scale_rows = [slice(QUAD_ROWS * quad, QUAD_ROWS * quad + PLANE_ROWS * PASSES) for quad in range(QUADS)]
        staged_scales = keep.tile([P, T // 4], I32, name="staged_scales")
        for quad, rows in enumerate(scale_rows):
            groups = slice(PLANE_ROWS * quad, PLANE_ROWS * (quad + 1))
            nc.gpsimd.dma_start(out=staged_scales[rows, :], in_=x_scales[:, groups, :].bitcast(I32))

        token_words = keep.tile([P, (PASSES - 1) * T + WINDOW], I32, name="token_words", align_bytes=64)
        nc.vector.memset(token_words[:, PASSES * T :], 0)
        nc.sync.dma_start(
            out=token_words[:, : PASSES * T].rearrange("p (o t) -> p o t", o=PASSES),
            in_=x_words.rearrange("o p t r -> p o (t r)").bitcast(I32),
        )
        slot_list = lists.tile([P, SLOTS // LIST_ROWS], U16, name="slot_list")
        nc.sync.dma_start(slot_list[:], offs)

        y = keep.tile([P, SLOTS + PAD], F32, name="y", align_bytes=64)
        nc.vector.memset(y[:, SLOTS:], 0.0)

        gate_all = keep.tile([P, TOP * T], F32, name="gate_all")
        gates = [gate_all[:, r * T : (r + 1) * T] for r in range(TOP)]

        held_gates = {}

        def spread_gate():
            blocks = T // P
            step = (N // blocks) * T + P
            start = (TOP - 1) * T
            pieces = gate.rearrange("r n t -> (r n t)")[start : start + TOP * blocks * step]
            staged_gate = keep.tile([TOP * blocks, P], F32, name="staged_gate")
            nc.sync.dma_start(out=staged_gate[:], in_=pieces.rearrange("(j s) -> j s", s=step)[:, :P])
            nc.scalar.copy(out=gate_rows[: TOP * blocks, :], in_=staged_gate[:])
            gate_turned = psum_y.tile([P, P], F32, name="gate_turned", tag="acc_y")
            nc.tensor.transpose(gate_turned[:], gate_rows[:], identity[:])
            gate_cols = keep.tile([P, TOP * blocks], F32, name="gate_cols")
            nc.scalar.copy(out=gate_cols[:], in_=gate_turned[:, : TOP * blocks])
            def spread_blocks(bank, first, count):
                for i in range(count):
                    nc.tensor.transpose(
                        bank[:, i * P : (i + 1) * P],
                        gate_cols[:, first + i : first + i + 1].to_broadcast([P, P]),
                        identity[:],
                    )

            turned_blocks = TOKEN_CUTS[1] // P
            runs = [(r * blocks, turned_blocks) for r in range(2)] + [(first, 4) for first in range(2 * blocks, TOP * blocks, 4)]
            for first, count in runs:
                spread = psum_y.tile([P, count * P], F32, name="spread", tag="acc_y")
                spread_blocks(spread, first, count)
                nc.scalar.copy(out=gate_all[:, first * P : (first + count) * P], in_=spread[:])
            cuts = (turned_blocks, turned_blocks + LAST_CUT // P, blocks)
            for i, (b0, b1) in enumerate(zip(cuts, cuts[1:])):
                held_gates[i] = psum_g.tile([P, 2, (b1 - b0) * P], F32, name="held_gate%d" % i)
                for r in range(2):
                    spread_blocks(held_gates[i][:, r, :], r * blocks + b0, b1 - b0)

        slot_words = keep.tile([P, PASSES, SLOTS], U32, name="slot_words", align_bytes=64)
        slot_scales = keep.tile([P, SLOTS], U8, name="slot_scales", align_bytes=64)

        def gather_words():
            for o in range(PASSES):
                window = token_words[:, o * T : o * T + WINDOW].bitcast(U32)
                nc.vector.tensor_copy(slot_words[:, o, :], window.indirect(slot_list[:]))

        def gather_scales():
            token_scales = ring_tile("token_scales", WINDOW, U8, W1_LOADS[0], 0)
            nc.vector.memset(token_scales.bitcast(I32), 0)
            for rows in scale_rows:
                nc.vector.tensor_copy(out=token_scales[rows, :T].bitcast(I32), in_=staged_scales[rows, :])
            nc.vector.tensor_copy(slot_scales[:], token_scales.indirect(slot_list[:]))

        w1_rows = w1.rearrange("e k c -> (e k) c")
        raw_passes = {}

        def load_w1(first, count):
            raw = ring_tile("raw%d" % first, count * PACK * H, F32, first % RING_SLOTS, 0)
            rows = w1_rows[first * P * PACK : (first + count) * P * PACK, :]
            nc.sync.dma_start(
                out=raw.rearrange("p (o x) -> p o x", o=count), in_=rows.rearrange("(o p j) c -> p o (j c)", p=P, j=PACK)
            )
            for i in range(count):
                raw_passes[first + i] = raw[:, i * PACK * H : (i + 1) * PACK * H]

        load_starts = {sum(W1_LOADS[:i]): count for i, count in enumerate(W1_LOADS)}

        sums, h_codes, h_scales, w2_codes, w2_scales = {}, {}, {}, {}, {}

        def round_w1(raw, w_bf, last):
            dst = w_bf.rearrange("p (t m j) -> p m j t", t=PACK, j=PACK)
            src = raw.rearrange("p (j m t) -> p m j t", j=PACK, t=PACK)
            if last:
                low, high = slice(0, PACK // 2), slice(PACK // 2, PACK)
                nc.vector.tensor_copy(out=dst[:, :, :, low], in_=src[:, :, :, low])
                nc.vector.tensor_copy(out=dst[:, :LAST_VECTOR_M, :, high], in_=src[:, :LAST_VECTOR_M, :, high])
                nc.scalar.copy(out=dst[:, LAST_VECTOR_M:, :, high], in_=src[:, LAST_VECTOR_M:, :, high])
            else:
                nc.vector.tensor_copy(out=dst[:, :VECTOR_M], in_=src[:, :VECTOR_M])
                nc.scalar.copy(out=dst[:, VECTOR_M:], in_=src[:, VECTOR_M:])

        def multiply(acc, slots, o, codes, scales):
            for t in range(PACK):
                cols = slice(t * P, (t + 1) * P)
                nc.tensor.matmul_mx(
                    out=acc[:, t, :],
                    lhsT=codes[:, cols].bitcast(FP8X4),
                    lhsT_scale=scales[:, cols],
                    rhs=slot_words[:, o, slots].bitcast(FP8X4),
                    rhs_scale=slot_scales[PLANE_ROWS * o :, slots],
                    start=(o == 0 and t == 0),
                    stop=(o == PASSES - 1 and t == PACK - 1),
                )

        waiting = []
        first_multiplied = sum(W1_LOADS[:2]) - 1

        def first_layer(e):
            slots = slice(e * C, (e + 1) * C)
            acc = psum_a.tile([P, PACK, C], F32, name="acc", tag="acc")
            for o in range(PASSES):
                g = e * PASSES + o
                if g not in raw_passes:
                    load_w1(g, load_starts[g])
                last = g == E * PASSES - 1
                if not last:
                    w_bf = rounded.tile([P, H * PACK], BF16, name="w1_bf", align_bytes=64)
                round_w1(raw_passes[g], w_bf[:], last)
                codes = coded.tile([P, H], U32, name="w1_codes", align_bytes=64)
                scales = coded.tile([P, H], U8, name="w1_scales", align_bytes=64)
                width = H // 2 if last else H
                for c0 in range(0, H, width):
                    nc.vector.quantize_mx(
                        out=codes[:, c0 : c0 + width].bitcast(FP8X4),
                        scales=scales[:, c0 : c0 + width],
                        in_=w_bf[:, c0 * PACK : (c0 + width) * PACK],
                    )
                waiting.append((acc, slots, o, codes, scales))
                if g == first_multiplied:
                    gather_scales()
                if g >= first_multiplied:
                    for job in waiting:
                        multiply(*job)
                    waiting.clear()
                if g + 1 in load_starts and g >= first_multiplied:
                    for done in range(e):
                        if done not in h_codes:
                            first_pass = (done + 1) * PASSES
                            activate(done, ring_tile("h%d" % done, H, BF16, first_pass % RING_SLOTS, 0))
            sums[e] = acc

        def activate(e, h_bf):
            nc.scalar.activation(
                out=h_bf.rearrange("p (s t) -> p s t", t=PACK), in_=sums[e][:].rearrange("p t s -> p s t"), func=SILU
            )
            h_codes[e] = keep.tile([P, C], U32, name="h_codes%d" % e, align_bytes=64)
            h_scales[e] = keep.tile([P, C], U8, name="h_scales%d" % e, align_bytes=64)
            nc.vector.quantize_mx(out=h_codes[e][:].bitcast(FP8X4), scales=h_scales[e][:], in_=h_bf)

        def load_w2(first, count, raw):
            nc.sync.dma_start(
                out=raw.rearrange("p (e x) -> p e x", x=H),
                in_=w2[first : first + count].rearrange("e (p j) n -> p e (j n)", j=PACK),
            )
            return raw

        def round_w2(raw, w_bf, copy, pieces=1):
            dst = w_bf.rearrange("p (e c i j) -> p e c j i", c=N // 4, i=4, j=PACK)
            src = raw.rearrange("p (e j c i) -> p e c j i", c=N // 4, i=4, j=PACK)
            step = N // 4 // pieces
            for c0 in range(0, N // 4, step):
                copy(out=dst[:, :, c0 : c0 + step], in_=src[:, :, c0 : c0 + step])

        def quantise_w2(first, count, w_bf, pieces=1):
            codes = keep.tile([P, count * N], U32, name="w2_codes%d" % first, align_bytes=64)
            scales = keep.tile([P, count * N], U8, name="w2_scales%d" % first, align_bytes=64)
            step = count * N // pieces
            for c0 in range(0, count * N, step):
                nc.vector.quantize_mx(
                    out=codes[:, c0 : c0 + step].bitcast(FP8X4),
                    scales=scales[:, c0 : c0 + step],
                    in_=w_bf[:, c0 * PACK : (c0 + step) * PACK],
                )
            for i in range(count):
                w2_codes[first + i] = codes[:, i * N : (i + 1) * N]
                w2_scales[first + i] = scales[:, i * N : (i + 1) * N]

        def second_layer(first, count):
            acc = psum_y.tile([P, count * C], F32, name="acc_y")
            for i in range(count):
                nc.tensor.matmul_mx(
                    out=acc[:, i * C : (i + 1) * C],
                    lhsT=w2_codes[first + i].bitcast(FP8X4),
                    lhsT_scale=w2_scales[first + i],
                    rhs=h_codes[first + i][:].bitcast(FP8X4),
                    rhs_scale=h_scales[first + i][:],
                    start=True,
                    stop=True,
                )
            return acc

        def put_results(first, count, acc):
            nc.scalar.copy(out=y[:, first * C : (first + count) * C], in_=acc[:])

        back_lists = {}

        def load_back_list(r):
            back_lists[r] = lists.tile([P, T // LIST_ROWS], U16, name="back%d" % r)
            nc.sync.dma_start(back_lists[r][:], (pos1, pos2, pos3, pos4)[r])

        load_w1(0, load_starts[0])
        spread_gate()
        gather_words()
        for e in range(E):
            first_layer(e)
            if e == EARLY_AT:
                early_raw = keep.tile([P, EARLY_W2 * H], F32, name="early_raw")
                early_bf = keep.tile([P, EARLY_W2 * H], BF16, name="w2_bf", align_bytes=64)
                round_w2(load_w2(0, EARLY_W2, early_raw[:]), early_bf[:], nc.scalar.copy)
                quantise_w2(0, EARLY_W2, early_bf[:])
                put_results(0, EARLY_W2, second_layer(0, EARLY_W2))
        last_h = keep.tile([P, H], BF16, name="last_h", align_bytes=64)

        def late_raw(first, count):
            byte = (first - EARLY_W2) * H * 4
            return load_w2(first, count, ring_tile("w2_raw%d" % first, count * H, F32, LATE_W2_SLOT, byte))

        def late_bf(first, count, place):
            return ring_tile("w2_bf%d" % first, count * H, BF16, (E * PASSES - 1) % RING_SLOTS, place * H * 2)

        bf23, bf45 = late_bf(2, 2, 0), late_bf(4, 2, 2)
        round_w2(late_raw(2, 2), bf23, nc.scalar.copy)
        round_w2(late_raw(4, 1), bf45[:, :H], nc.vector.tensor_copy)
        round_w2(late_raw(5, 1), bf45[:, H:], nc.vector.tensor_copy)
        quantise_w2(2, 2, bf23)
        quantise_w2(4, 2, bf45)
        acc23, acc45 = second_layer(2, 2), second_layer(4, 2)
        activate(E - 1, last_h[:])
        bf6, bf7 = late_bf(6, 1, 0), late_bf(7, 1, 1)
        round_w2(late_raw(6, 1), bf6, nc.scalar.copy)
        round_w2(late_raw(7, 1), bf7, nc.vector.tensor_copy, pieces=2)
        for r in (3, 2, 0, 1):
            load_back_list(r)
        put_results(2, 2, acc23)
        put_results(4, 2, acc45)
        quantise_w2(6, 1, bf6)
        put_results(6, 1, second_layer(6, 1))
        quantise_w2(7, 1, bf7, pieces=2)
        put_results(7, 1, second_layer(7, 1))

        def part_tile(name, ring_slot, lo, hi, r, lists=1):
            return ring_tile("%s%d_%d" % (name, lo, r), lists * (hi - lo), F32, ring_slot, 4 * (TOP * lo + r * (hi - lo)))

        def offsets(lo, hi, r):
            return back_lists[r][:, lo // LIST_ROWS : hi // LIST_ROWS]

        def fetch(lo, hi, r, part):
            nc.vector.tensor_tensor(part, y[:].indirect(offsets(lo, hi, r)), gates[r][:, lo:hi], MULT)
            return part

        def pick(lo, hi, r, picked):
            nc.scalar.activation(picked, y[:].indirect(offsets(lo, hi, r)), COPY)
            return picked

        def turn_and_sum(cols, parts):
            turned = psum_y.tile([P, P], F32, name="acc_y")
            for i, part in enumerate(parts):
                nc.tensor.matmul(
                    turned[:], lhsT=part[:, cols], rhs=identity[:], is_transpose=True, start=(i == 0), stop=(i == TOP - 1)
                )
            by_token = keep.tile([P, P], F32, name="by_token%d" % cols.start)
            nc.scalar.copy(out=by_token[:], in_=turned[:])
            return by_token

        def turn_back(by_token, total, pool, tag):
            upright = pool.tile([P, P], F32, name="upright", tag=tag)
            nc.tensor.transpose(upright[:], by_token[:], identity[:])
            nc.scalar.copy(out=total, in_=upright[:])

        def add(name, a, b):
            total = keep.tile([P, a.shape[1]], F32, name=name)
            nc.vector.tensor_tensor(total[:], a, b, ADD)
            return total[:]

        def weigh(picked, weights, part):
            nc.vector.tensor_tensor(part, picked, weights, MULT)
            return part

        first, lo, hi = TOKEN_CUTS
        width = hi - lo
        picked = part_tile("picked", PICKED_SLOT, first, lo, 0, lists=3)
        pieces = [slice(first, FIRST_PICK), slice(FIRST_PICK, lo)]
        for cols in pieces:
            pick(cols.start, cols.stop, 0, picked[:, cols])
        picked_last = part_tile("picked", PICKED_SLOT, lo, hi, 0, lists=2)
        for r in range(2):
            pick(lo, hi, r, picked_last[:, r * width : (r + 1) * width])
        wide = [fetch(first, lo, r, part_tile("part", PARTS_SLOT, first, lo, r)) for r in (3, 2)]
        wide.append(part_tile("weighed", WEIGHED_SLOT, first, lo, 0))
        for cols in pieces:
            weigh(picked[:, cols], gates[0][:, cols], wide[2][:, cols])
        wide.append(fetch(first, lo, 1, part_tile("part", PARTS_SLOT, first, lo, 1)))
        blocks = [slice(b, b + P) for b in range(first, lo, P)]
        sums_by_token = [turn_and_sum(cols, wide) for cols in blocks]
        turned_total = keep.tile([P, lo - first], F32, name="turned_total")
        for cols, by_token, bank in zip(blocks, sums_by_token, ((psum_a, "acc"), (psum_a, "acc"), (psum_y, "acc_y"))):
            turn_back(by_token, turned_total[:, cols], *bank)
        nc.scalar.dma_start(out=out[:, first:lo], in_=turned_total[:])

        p3 = fetch(lo, hi, 3, part_tile("last", PICKED_SLOT, first, lo, 0))
        p2 = fetch(lo, hi, 2, part_tile("last", PICKED_SLOT, first, lo, 1))
        halves = [slice(0, LAST_CUT), slice(LAST_CUT, width)]
        s23 = [
            keep.tile([P, LAST_CUT], F32, name="s23")[:],
            part_tile("s23", PICKED_SLOT, lo, hi, 1)[:, : width - LAST_CUT],
        ]
        nc.gpsimd.tensor_tensor(s23[0], p2[:, halves[0]], p3[:, halves[0]], ADD)
        products = [
            ring_tile("products0", 2 * LAST_CUT, F32, PICKED_SLOT, 4 * 2 * (lo - first)),
            ring_tile("products1", 2 * (width - LAST_CUT), F32, WEIGHED_SLOT + 1, 0),
        ]
        products = [both.rearrange("p (r t) -> p r t", r=2) for both in products]
        for i, cols in enumerate(halves):
            weigh(picked_last.rearrange("p (r t) -> p r t", r=2)[:, :, cols], held_gates[i][:], products[i])
        s01 = [add("s01_0", products[0][:, 0, :], products[0][:, 1, :])]
        nc.vector.tensor_tensor(s23[1], p2[:, halves[1]], p3[:, halves[1]], ADD)
        s01.append(add("s01_1", products[1][:, 0, :], products[1][:, 1, :]))
        for i, cols in enumerate(halves):
            total = add("s0123_%d" % i, s01[i], s23[i])
            nc.sync.dma_start(out=out[:, lo + cols.start : lo + cols.stop], in_=total)
